import numpy as np
import ml_dtypes


def mxq(x, axis, fmt="e4m3"):
    dtype, down = {"e4m3": (ml_dtypes.float8_e4m3fn, 7), "e5m2": (ml_dtypes.float8_e5m2, 14)}[fmt]
    v = np.moveaxis(np.asarray(x, np.float32).astype(ml_dtypes.bfloat16).astype(np.float64), axis, -1)
    blocks = v.reshape(v.shape[:-1] + (-1, 32))
    amax = np.abs(blocks).max(-1, keepdims=True)
    byte = np.maximum(np.where(amax > 0, np.frexp(amax)[1] - 1 + 127, 0) - down, 1)
    scale = np.exp2(byte - 127.0)
    codes = (blocks / scale).astype(np.float32).astype(dtype).astype(np.float64)
    return np.moveaxis((codes * scale).reshape(v.shape), -1, axis)


WIDE = False


def mx_kscale(k):
    if not WIDE:
        return np.ones(k)
    levels = np.array([10, -10, 5, -5, 0])
    if k % 512:
        return np.exp2(np.random.permutation(np.resize(levels, k // 32))).repeat(32)
    a = np.empty((k // 512, 16))
    for p in range(k // 512):
        a[p, :8] = np.random.permutation(np.resize(levels, 8))
        for g in range(8):
            far = levels[np.abs(levels - a[p, g]) >= 10]
            a[p, g + 8] = far[np.random.randint(len(far))]
    return np.exp2(a.ravel()).repeat(32)


BF16 = ml_dtypes.bfloat16


def bf(x):
    return np.asarray(x, np.float32).astype(BF16)


def f64(x):
    return np.asarray(x).astype(np.float64)

def planes(Y):
    n, m = Y.shape
    b = f64(bf(Y)).reshape(n // 32, 32, m)
    amax = np.abs(b).max(1)
    byte = np.clip(np.where(amax > 0, np.frexp(amax)[1] - 1 + 127 - 7, 1), 1, 254)
    codes = (b * np.exp2(127.0 - byte)[:, None, :]).reshape(n, m).astype(np.float32).astype(ml_dtypes.float8_e4m3fn).view(np.uint8)
    words = codes.reshape(n // 512, 128, 4, m).transpose(0, 1, 3, 2)
    return np.ascontiguousarray(words), np.ascontiguousarray(byte.astype(np.uint8).reshape(n // 512, 16, m))


Q, N, D, F = 64, 32, 512, 1024
TEMPERATURE = 0.5
LOSS_SCALE = 256.0


def sigmoid(v):
    return 1.0 / (1.0 + np.exp(-v))


def pairwise_soft_order(s):
    return sigmoid((s[:, None, :] - s[:, :, None]) / TEMPERATURE)


def rank_gradient(rank, gain):
    one_plus = 1.0 + rank
    log_term = np.log(one_plus)
    return gain * np.log(2.0) / (one_plus * (log_term * log_term))


def score_gradient(c, k):
    diff = c[:, :, None] - c[:, None, :]
    return (LOSS_SCALE / TEMPERATURE) * np.sum(diff * k * (1.0 - k), axis=1)


def setup_inputs():
    u, t = mx_kscale(D), mx_kscale(F)
    return {
        "x": bf(np.random.standard_normal((Q, N, D))),
        "gamma": bf((1.0 + 0.1 * np.random.standard_normal(D)) * u),
        "w1": bf(np.random.standard_normal((D, F)) / np.sqrt(D) / u[:, None] * t[None, :]),
        "g1": bf((1.0 + 0.1 * np.random.standard_normal(F)) / t),
        "w2": bf(2.0 * np.random.standard_normal(F) / np.sqrt(F)),
        "gain": bf(np.random.uniform(0.0, 1.0, (Q, N))),
    }


def core(x, gamma, w1, g1, w2, gain):
    x, gamma, w1, g1, w2, gain = f64(x), f64(gamma), f64(w1), f64(g1), f64(w2), f64(gain)
    p = mxq(x * gamma, 2, "e4m3") @ mxq(w1, 0, "e4m3")
    a = p * g1
    sg = sigmoid(a)
    s = np.sum(a * sg * w2, axis=-1)
    k = pairwise_soft_order(s)
    rank = 0.5 + np.sum(k, axis=2)
    c = rank_gradient(rank, gain)
    delta = score_gradient(c, k)
    dp = delta[:, :, None] * w2 * sg * (1.0 + a * (1.0 - sg)) * g1
    dz = mxq(dp, 2, "e4m3") @ mxq(w1, 1, "e4m3").T
    return dz * gamma


def reference(x, gamma, w1, g1, w2, gain):
    R_out = core(x, gamma, w1, g1, w2, gain)
    words, scales = planes(np.moveaxis(R_out, 2, 0).reshape(512, -1))
    return R_out, words, scales

@@ -1,0 +1,604 @@
+import math
+from contextlib import ExitStack
+
+import concourse.mybir as mybir
+from concourse.masks import make_identity
+
+F32 = mybir.dt.float32
+BF16 = mybir.dt.bfloat16
+U32 = mybir.dt.uint32
+I32 = mybir.dt.int32
+U8 = mybir.dt.uint8
+FP8X4 = mybir.dt.float8_e4m3fn_x4
+ACT = mybir.ActivationFunctionType
+ALU = mybir.AluOpType
+AX = mybir.AxisListType
+
+ROWS, D, F = 2048, 512, 1024
+FLOPS = 4 * ROWS * D * F
+NB = 4
+MPRIME = ((2, 1), (3, 0), (3, 1))
+PBUF = 3
+QBUF = 6
+N3_GPS = False
+YI = ("g", "g", "g", "v")
+MP_AT = [((2, 1), 64), ((3, 0), 70), ((3, 1), 74)]
+PAIR_AT = (39, 39, 39, 42, 44, 46)
+PAIRB_AT = (65, 67, 67, 70, 72, 74)
+WT_AT = 33
+X_AT = (1, 10, 22)
+U_AT = [48 + i for i in range(16)] + [78 + i for i in range(4)] + [83, 86, 89]
+L_AT = (65, 74, 86, 92)
+
+def tile_smoothedrankdcginputgradient_kernel(tc, x, gamma, w1, g1, w2, gain, out_0, out_1, out_2):
+    nc = tc.nc
+    xr = x.rearrange("q n d -> (q n) d")
+    yr = out_0.rearrange("q n d -> (q n) d")
+    words_out = out_1.rearrange("g p m t -> g p (m t)")
+
+    with ExitStack() as ctx:
+        keep = ctx.enter_context(tc.tile_pool(name="keep", bufs=1))
+        work = ctx.enter_context(tc.tile_pool(name="work", bufs=2))
+        pairp = ctx.enter_context(tc.tile_pool(name="pairp", bufs=1))
+        pp = ctx.enter_context(tc.psum_pool(name="pp", bufs=PBUF))
+        pt = ctx.enter_context(tc.psum_pool(name="pt", bufs=2))
+        pc = ctx.enter_context(tc.psum_pool(name="pc", bufs=2))
+        ps = ctx.enter_context(tc.psum_pool(name="ps", bufs=1))
+        ctx.enter_context(tc.manual_schedule())
+
+        gz = keep.tile([128, D], BF16, name="gz")
+        nc.vector.memset(gz[:], 0.0)
+        ones = keep.tile([128, 128], BF16, name="ones")
+        nc.vector.memset(ones[:], 1.0)
+        nc.scalar.dma_start(out=gz[0:1, :], in_=gamma.unsqueeze(0))
+        w1raw = keep.tile([128, 4, F], BF16, name="w1raw")
+        xb = []
+        for b in range(NB):
+            xt = keep.tile([128, 4, D], BF16, name="xb%d" % b)
+            xb.append(xt)
+
+        def load_x(b, half):
+            r0 = 512 * b + 256 * half
+            nc.sync.dma_start(out=xb[b][:, 2 * half:2 * half + 2, :], in_=xr[r0:r0 + 256, :].rearrange("(k p) d -> p k d", p=128))
+
+        def load_w(g):
+            nc.sync.dma_start(out=w1raw[:, :, 512 * g:512 * g + 512], in_=w1[:, 512 * g:512 * g + 512].rearrange("(p j) f -> p j f", j=4))
+
+        load_x(0, 0)
+        load_w(0)
+        load_x(0, 1)
+        load_w(1)
+        g1b = keep.tile([128, 2, 4], BF16, name="g1b")
+        nc.scalar.dma_start(out=g1b[:], in_=g1.rearrange("(g p t) -> p g t", g=2, t=4))
+        w2b = keep.tile([128, 2, 4], BF16, name="w2b")
+        nc.scalar.dma_start(out=w2b[:], in_=w2.rearrange("(g p t) -> p g t", g=2, t=4))
+        gmb = keep.tile([128, 4], BF16, name="gmb")
+        nc.scalar.dma_start(out=gmb[:], in_=gamma.rearrange("(p t) -> p t", t=4))
+        for b in (1, 2, 3):
+            load_x(b, 0)
+            load_x(b, 1)
+
+        identf = keep.tile([128, 128], F32, name="identf")
+        make_identity(nc, identf[:])
+        blk = keep.tile([128, 128], F32, name="blk")
+        nc.gpsimd.memset(blk[:], 0.0)
+        for q in range(4):
+            nc.gpsimd.memset(blk[32 * q:32 * q + 32, 32 * q:32 * q + 32], 1.0)
+        gainz = keep.tile([128, 128], BF16, name="gainz")
+        nc.gpsimd.memset(gainz[:], 0.0)
+        identb = keep.tile([128, 128], BF16, name="identb")
+        nc.gpsimd.tensor_scalar(out=identb[:], in0=identf[:], scalar1=1.0, scalar2=0.0, op0=ALU.mult, op1=ALU.add)
+        nc.sync.dma_start(out=gainz[0:16, :], in_=gain.rearrange("(a q) n -> a (q n)", q=4))
+        g1r = work.tile([64, F], BF16, name="g1r", tag="yi", align_bytes=64)
+        w2r = work.tile([64, F], BF16, name="w2r", tag="yi", align_bytes=64)
+        nc.gpsimd.memset(g1r[:], 0.0)
+        nc.gpsimd.memset(w2r[:], 0.0)
+        for r0 in (0, 32):
+            nc.sync.dma_start(out=g1r[r0:r0 + 3, :], in_=g1.partition_broadcast(3))
+            nc.sync.dma_start(out=w2r[r0:r0 + 3, :], in_=w2.partition_broadcast(3))
+        crow = keep.tile([128, 8, 128], BF16, name="crow")
+        nc.gpsimd.memset(crow[:], 0.0)
+        dparts = keep.tile([128, 16, 128], BF16, name="dparts")
+        nc.gpsimd.memset(dparts[:], 0.0)
+        orow = keep.tile([128, 128], BF16, name="orow")
+        nc.gpsimd.memset(orow[:], 0.0)
+        nc.gpsimd.memset(orow[0:32, :], 1.0)
+        c_f = work.tile([64, F], F32, name="c_f", tag="yt")
+        nc.gpsimd.tensor_tensor(out=c_f[:], in0=g1r[:], in1=w2r[:], op=ALU.mult)
+        c_hi = work.tile([64, F], BF16, name="c_hi", tag="yt")
+        nc.gpsimd.tensor_scalar(out=c_hi[:], in0=c_f[:], scalar1=1.0, scalar2=0.0, op0=ALU.mult, op1=ALU.add)
+        c_lo = work.tile([64, F], BF16, name="c_lo", tag="dpi", align_bytes=64)
+        nc.gpsimd.tensor_tensor(out=c_lo[:], in0=c_f[:], in1=c_hi[:], op=ALU.subtract)
+        for g in range(2):
+            for r0, src in ((0, c_hi), (32, c_lo)):
+                nc.gpsimd.tensor_scalar(
+                    out=crow[r0:r0 + 32, 4 * g:4 * g + 4, :],
+                    in0=src[r0:r0 + 32, 512 * g:512 * g + 512].rearrange("k (m t) -> k t m", t=4),
+                    scalar1=1.0, scalar2=0.0, op0=ALU.mult, op1=ALU.add)
+
+        warm = keep.tile([128, 1], F32, name="warm")
+        nc.scalar.activation(out=warm[:], in_=ones[:, 0:1], func=ACT.Silu)
+
+        gps = pt.tile([128, D], F32, name="tp")
+        nc.tensor.matmul(gps[:], lhsT=ones[:], rhs=gz[:], start=True, stop=True)
+        gbc = keep.tile([128, D], BF16, name="gbc")
+        nc.vector.tensor_copy(out=gbc[:], in_=gps[:])
+
+        w1c = keep.tile([128, 2, 512], U32, name="w1c", align_bytes=64)
+        w1s = keep.tile([128, 2, 512], U8, name="w1s", align_bytes=64)
+        wtc = keep.tile([128, 2, 512], U32, name="wtc", align_bytes=64)
+        wts = keep.tile([128, 2, 512], U8, name="wts", align_bytes=64)
+        xc = []
+        xs = []
+        for b in range(NB):
+            t1 = keep.tile([128, 512], U32, name="xc%d" % b, align_bytes=64)
+            t2 = keep.tile([128, 512], U8, name="xs%d" % b, align_bytes=64)
+            xc.append(t1)
+            xs.append(t2)
+        xg = {}
+        xi = {}
+        ttile = {}
+
+        def x_mul(b, half):
+            t = work.tile([128, 2, D], BF16, name="xg")
+            nc.vector.tensor_tensor(out=t[:], in0=xb[b][:, 2 * half:2 * half + 2, :],
+                                    in1=gbc[:].unsqueeze(1).to_broadcast([128, 2, D]), op=ALU.mult)
+            xg[b, half] = t
+
+        def x_turn(b, half):
+            t = pt.tile([128, 2, 2, 128], F32, name="tp")
+            words = xg[b, half][:].bitcast(F32)
+            for k in range(2):
+                for u in range(2):
+                    nc.tensor.transpose(t[:, k, u, :], words[:, k, u:256:2], identf[:])
+            ttile[b, half] = t
+
+        def x_copy(b, half, eng):
+            if half == 0:
+                t = work.tile([128, 2048], BF16, name="xi", align_bytes=64)
+                xi[b] = t
+            dst = xi[b][:, 1024 * half:1024 * half + 1024].bitcast(F32).rearrange("p (k r u) -> p k r u", k=2, u=2)
+            src = ttile[b, half][:].rearrange("p k u r -> p k r u")
+            if eng == "v":
+                nc.vector.tensor_copy(out=dst, in_=src)
+            else:
+                nc.scalar.copy(out=dst, in_=src)
+
+        def x_quant(b):
+            nc.vector.quantize_mx(out=xc[b][:].bitcast(FP8X4), scales=xs[b][:], in_=xi[b][:])
+
+        wi = {}
+
+        def w_inter(g, eng):
+            t = work.tile([128, 2048], BF16, name="wi", align_bytes=64)
+            wi[g] = t
+            dst = t[:].rearrange("p (t m j) -> p t m j", t=4, j=4)
+            src = w1raw[:, :, 512 * g:512 * g + 512].rearrange("p j (m t) -> p t m j", t=4)
+            for t2 in range(4):
+                if eng == "v":
+                    nc.vector.tensor_copy(out=dst[:, t2, :, :], in_=src[:, t2, :, :])
+                else:
+                    nc.scalar.copy(out=dst[:, t2, :, :], in_=src[:, t2, :, :])
+
+        def w_quant(g):
+            nc.vector.quantize_mx(out=w1c[:, g, :].bitcast(FP8X4), scales=w1s[:, g, :], in_=wi[g][:])
+
+        def wt_turn(g, half):
+            t = pt.tile([128, 2, 2, 128], F32, name="tp")
+            for k in range(2):
+                words = w1raw[:, 2 * half + k, :].bitcast(F32)
+                for u in range(2):
+                    nc.tensor.transpose(t[:, k, u, :], words[:, 256 * g + u:256 * g + 256:2], identf[:])
+            ttile["w", g, half] = t
+
+        def wt_copy(g, half):
+            if half == 0:
+                t = work.tile([128, 2048], BF16, name="wi", align_bytes=64)
+                wi["t", g] = t
+            dst = wi["t", g][:, 1024 * half:1024 * half + 1024].bitcast(F32).rearrange("p (k m u) -> p k m u", k=2, u=2)
+            nc.vector.tensor_copy(out=dst, in_=ttile["w", g, half][:].rearrange("p k u m -> p k m u"))
+
+        def wt_quant(g):
+            nc.vector.quantize_mx(out=wtc[:, g, :].bitcast(FP8X4), scales=wts[:, g, :], in_=wi["t", g][:])
+
+        x_mul(0, 0)
+        w_inter(0, "v")
+        x_turn(0, 0)
+        x_mul(0, 1)
+        w_quant(0)
+        x_copy(0, 0, "s")
+        x_turn(0, 1)
+        x_copy(0, 1, "v")
+        x_quant(0)
+        w_inter(1, "s")
+        g1c = keep.tile([128, 8], F32, name="g1c")
+        nc.vector.tensor_copy(out=g1c[:], in_=g1b[:].rearrange("p g t -> p (g t)"))
+        ng1c = keep.tile([128, 8], F32, name="ng1c")
+        nc.vector.tensor_scalar_mul(out=ng1c[:], in0=g1c[:], scalar1=-1.0)
+        hg1c = keep.tile([128, 8], F32, name="hg1c")
+        nc.vector.tensor_scalar_mul(out=hg1c[:], in0=g1c[:], scalar1=0.5)
+        w_quant(1)
+        w2c = keep.tile([128, 8], F32, name="w2c")
+        nc.vector.tensor_copy(out=w2c[:], in_=w2b[:].rearrange("p g t -> p (g t)"))
+        gmc = keep.tile([128, 4], F32, name="gmc")
+        nc.vector.tensor_copy(out=gmc[:], in_=gmb[:])
+        c8 = keep.tile([128, 8], F32, name="c8")
+        nc.vector.tensor_tensor(out=c8[:], in0=g1c[:], in1=w2c[:], op=ALU.mult)
+
+        ecol = keep.tile([128, 32], F32, name="ecol")
+        gainc = keep.tile([128, 16], F32, name="gainc")
+
+        def consts():
+            nc.vector.tensor_reduce(out=ecol[:], in_=identf[:].rearrange("p (a i) -> p i a", i=32), axis=AX.X, op=ALU.add)
+            t = pt.tile([128, 128], BF16, name="tp")
+            nc.tensor.transpose(t[:], gainz[:], identb[:])
+            nc.vector.tensor_copy(out=gainc[:], in_=t[:, 0:16])
+
+        acts = []
+        for b in (0, 1):
+            for ft in range(8):
+                acts.append(("silu", b, ft))
+                acts.append(("tanh", b, ft))
+        for ft in range(8):
+            acts.append(("sig", 2, ft))
+        for ft in range(7, -1, -1):
+            acts.append(("silu", 2, ft))
+        for ft in range(8):
+            acts.append(("silu", 3, ft))
+        for ft in range(7, -1, -1):
+            acts.append(("sig", 3, ft))
+        tiles = []
+        where = {}
+        for i, (kind, b, ft) in enumerate(acts):
+            kept = b < 2 or ft >= 8 - PBUF
+            if (b, ft) in where and kept:
+                m = where[b, ft]
+                tiles[m] = (b, ft, i)
+            else:
+                where[b, ft] = len(tiles)
+                tiles.append((b, ft, i))
+        acc = {}
+
+        def stage1(m):
+            b, ft, last = tiles[m]
+            g, t = divmod(ft, 4)
+            p = pp.tile([128, 512], F32, name="p")
+            nc.tensor.matmul_mx(p[:], lhsT=w1c[:, g, 128 * t:128 * t + 128].bitcast(FP8X4), lhsT_scale=w1s[:, g, 128 * t:128 * t + 128],
+                                rhs=xc[b][:].bitcast(FP8X4), rhs_scale=xs[b][:], start=True, stop=True)
+            acc[b, ft] = p
+
+        hn = {}
+        qn = {}
+
+        def act(i):
+            kind, b, ft = acts[i]
+            g, t = divmod(ft, 4)
+            if kind == "silu":
+                if (b, g) not in hn:
+                    h_t = work.tile([128, 4, 512], F32, name="h", bufs=4)
+                    hn[b, g] = h_t
+                nc.scalar.activation(out=hn[b, g][:, t, :], in_=acc[b, ft][:], func=ACT.Silu, scale=g1c[:, ft:ft + 1])
+                return
+            if (b, g) not in qn:
+                q = work.tile([128, 4, 512], F32, name="q", bufs=QBUF)
+                qn[b, g] = q
+            dst = qn[b, g][:, t, :]
+            if kind == "tanh":
+                nc.scalar.activation(out=dst, in_=acc[b, ft][:], func=ACT.Tanh, scale=hg1c[:, ft:ft + 1])
+            else:
+                nc.scalar.activation(out=dst, in_=acc[b, ft][:], func=ACT.Sigmoid, scale=ng1c[:, ft:ft + 1])
+
+        def q_op(b, k):
+            g, t = divmod(2 * k, 4)
+            q = qn[b, g][:, t:t + 2, :]
+            nc.vector.tensor_scalar(out=q, in0=q, scalar1=-0.5, scalar2=0.5, op0=ALU.mult, op1=ALU.add)
+
+        def n_op(b, k):
+            g, t = divmod(2 * k, 4)
+            q = qn[b, g][:, t:t + 2, :]
+            nc.vector.scalar_tensor_tensor(out=q, in0=hn[b, g][:, t:t + 2, :], scalar=1.0, in1=q, op0=ALU.subtract, op1=ALU.mult)
+
+        def n_gps(b, k):
+            g, t = divmod(2 * k, 4)
+            for j in range(2):
+                q = qn[b, g][:, t + j, :]
+                h_t = hn[b, g][:, t + j, :]
+                nc.gpsimd.tensor_scalar(out=h_t, in0=h_t, scalar1=1.0, scalar2=-1.0, op0=ALU.mult, op1=ALU.add)
+                nc.gpsimd.tensor_tensor(out=q, in0=h_t, in1=q, op=ALU.mult)
+
+        sps = {}
+
+        def s_mm(b, k, ft):
+            h = b // 2
+            if b % 2 == 0 and k == 0 and ft == 0:
+                t = ps.tile([128, 8], F32, name="sp")
+                sps[h] = t
+            g, t = divmod(ft, 4)
+            j = 4 * (b % 2) + k
+            nc.tensor.matmul(sps[h][:, j:j + 1], lhsT=hn[b, g][:, t, 128 * k:128 * k + 128], rhs=w2c[:, ft:ft + 1],
+                             start=(ft == 0), stop=(ft == 7))
+
+        st = {}
+
+        def bc(ap):
+            return ap.unsqueeze(2).to_broadcast([128, 8, 32])
+
+        def pair_bank(h, shape, dtype):
+            if h == 0:
+                bank = pc.tile(shape, dtype, name="c")
+            else:
+                bank = ps.tile(shape, dtype, name="sp")
+            return bank
+
+        def pair1(h):
+            s = pairp.tile([128, 8], F32, name="s")
+            nc.vector.tensor_copy(out=s[:], in_=sps[h][:])
+            se = pairp.tile([128, 8, 32], F32, name="se")
+            nc.vector.tensor_tensor(out=se[:], in0=bc(s[:]), in1=ecol[:].unsqueeze(1).to_broadcast([128, 8, 32]), op=ALU.mult)
+            r = ps.tile([128, 256], F32, name="sp")
+            nc.tensor.matmul(r[:], lhsT=blk[:], rhs=se[:].rearrange("p a i -> p (a i)"), start=True, stop=True)
+            st[h] = {"s": s, "r": r}
+
+        def pair2(h):
+            d = st[h]
+            df = pairp.tile([128, 8, 32], F32, name="df")
+            nc.vector.tensor_tensor(out=df[:], in0=d["r"][:].rearrange("p (a i) -> p a i", i=32), in1=bc(d["s"][:]), op=ALU.subtract)
+            kk = pairp.tile([128, 8, 32], F32, name="kk")
+            nc.scalar.activation(out=kk[:], in_=df[:], func=ACT.Sigmoid, scale=2.0)
+            kn = pairp.tile([128, 8, 32], F32, name="kn")
+            nc.scalar.activation(out=kn[:], in_=df[:], func=ACT.Sigmoid, scale=-2.0)
+            d["kk"] = kk
+            d["kn"] = kn
+
+        def pair3(h):
+            d = st[h]
+            u = pairp.tile([128, 8], F32, name="u")
+            nc.vector.tensor_reduce(out=u[:], in_=d["kk"][:], axis=AX.X, op=ALU.add)
+            u2 = pairp.tile([128, 8], F32, name="u2")
+            nc.vector.tensor_scalar_add(out=u2[:], in0=u[:], scalar1=1.5)
+            ln = pairp.tile([128, 8], F32, name="ln")
+            nc.scalar.activation(out=ln[:], in_=u2[:], func=ACT.Ln)
+            kp = pairp.tile([128, 8, 32], F32, name="kp")
+            nc.vector.tensor_tensor(out=kp[:], in0=d["kk"][:], in1=d["kn"][:], op=ALU.mult)
+            d["u2"] = u2
+            d["ln"] = ln
+            d["kp"] = kp
+
+        def pair4(h):
+            d = st[h]
+            t1 = pairp.tile([128, 8], F32, name="t1")
+            nc.vector.tensor_tensor(out=t1[:], in0=d["ln"][:], in1=d["ln"][:], op=ALU.mult)
+            t2 = pairp.tile([128, 8], F32, name="t2")
+            nc.vector.tensor_tensor(out=t2[:], in0=t1[:], in1=d["u2"][:], op=ALU.mult)
+            t3 = pairp.tile([128, 8], F32, name="t3")
+            nc.vector.reciprocal(out=t3[:], in_=t2[:])
+            cc = pairp.tile([128, 8], F32, name="cc")
+            nc.vector.scalar_tensor_tensor(out=cc[:], in0=t3[:], scalar=512.0 * math.log(2.0), in1=gainc[:, 8 * h:8 * h + 8], op0=ALU.mult, op1=ALU.mult)
+            ce = pairp.tile([128, 8, 32], F32, name="ce")
+            nc.vector.tensor_tensor(out=ce[:], in0=bc(cc[:]), in1=ecol[:].unsqueeze(1).to_broadcast([128, 8, 32]), op=ALU.mult)
+            r = ps.tile([128, 256], F32, name="sp")
+            nc.tensor.matmul(r[:], lhsT=blk[:], rhs=ce[:].rearrange("p a i -> p (a i)"), start=True, stop=True)
+            d["cc"] = cc
+            d["cr"] = r
+
+        dt_ = {}
+
+        def pair5(h):
+            d = st[h]
+            z1 = pairp.tile([128, 8, 32], F32, name="z1")
+            nc.vector.tensor_tensor(out=z1[:], in0=d["cr"][:].rearrange("p (a i) -> p a i", i=32), in1=bc(d["cc"][:]), op=ALU.subtract)
+            z2 = pairp.tile([128, 8, 32], F32, name="z2")
+            nc.vector.tensor_tensor(out=z2[:], in0=z1[:], in1=d["kp"][:], op=ALU.mult)
+            de = pairp.tile([128, 8, 1], F32, name="de")
+            nc.vector.tensor_reduce(out=de[:].rearrange("p a o -> p (a o)"), in_=z2[:], axis=AX.X, op=ALU.add)
+            cur = de
+            for k in range(3):
+                part = dparts[:, 8 * h:8 * h + 8, k:64:32]
+                nc.vector.tensor_copy(out=part, in_=cur[:].to_broadcast([128, 8, 2]))
+                if k < 2:
+                    nxt = pairp.tile([128, 8, 1], F32, name="de%d" % k)
+                    nc.vector.tensor_tensor(out=nxt[:], in0=cur[:], in1=dparts[:, 8 * h:8 * h + 8, k:k + 1], op=ALU.subtract)
+                    cur = nxt
+            t = ps.tile([128, 1024], BF16, name="sp")
+            for k in range(8):
+                nc.tensor.transpose(t[:, 128 * k:128 * k + 128], dparts[:, 8 * h + k, :], identb[:])
+            dt_[h] = t
+
+        dd = keep.tile([128, ROWS], BF16, name="dd")
+
+        def pair6(h):
+            nc.vector.tensor_copy(out=dd[:, 1024 * h:1024 * h + 1024], in_=dt_[h][:])
+
+        units = []
+        for b in range(NB):
+            for g in range(2):
+                if (b, g) in MPRIME:
+                    units.append((b, g, None))
+                else:
+                    for k in range(4):
+                        units.append((b, g, k))
+        cbank = {}
+
+        def delta_c(i):
+            if i >= len(units):
+                return
+            b, g, k = units[i]
+            if k is None and g == 1 and (b, 0) in MPRIME:
+                cbank[i] = cbank[i - 1]
+                return
+            c0 = 512 * b
+            if k is None:
+                t = pc.tile([128, 512], F32, name="c")
+                nc.tensor.matmul(t[:], lhsT=orow[:], rhs=dd[:, c0:c0 + 512], start=True, stop=True)
+            else:
+                t = pc.tile([128, 4, 128], F32, name="c")
+                for j in range(4):
+                    nc.tensor.matmul(t[:, j, :], lhsT=crow[:, 4 * g + j, :], rhs=dd[:, c0 + 128 * k:c0 + 128 * k + 128], start=True, stop=True)
+            cbank[i] = t
+
+        dpi = {}
+        dpc = {}
+
+        def m_prime(b, g):
+            for t in range(4):
+                hv = qn[b, g][:, t, :]
+                nc.scalar.activation(out=hv, in_=hv, func=ACT.Identity, scale=c8[:, 4 * g + t:4 * g + t + 1], bias=c8[:, 4 * g + t:4 * g + t + 1])
+
+        def dp_op(i):
+            b, g, k = units[i]
+            if k is None or k == 0:
+                t = work.tile([128, 2048], BF16, name="dpi", align_bytes=64)
+                dpi[b, g] = t
+            if k is None:
+                nc.vector.tensor_tensor(out=dpi[b, g][:].rearrange("p (r t) -> p r t", t=4), in0=qn[b, g][:].rearrange("p t r -> p r t"),
+                                        in1=cbank[i][:].unsqueeze(2).to_broadcast([128, 512, 4]), op=ALU.mult)
+            else:
+                nc.vector.scalar_tensor_tensor(
+                    out=dpi[b, g][:, 512 * k:512 * k + 512].rearrange("p (r t) -> p r t", t=4),
+                    in0=qn[b, g][:, :, 128 * k:128 * k + 128].rearrange("p t r -> p r t"), scalar=1.0,
+                    in1=cbank[i][:].rearrange("p t r -> p r t"), op0=ALU.add, op1=ALU.mult)
+
+        def dp_quant(b, g):
+            c = work.tile([128, 512], U32, name="dpc", align_bytes=64, bufs=4)
+            s = work.tile([128, 512], U8, name="dps", align_bytes=64, bufs=4)
+            nc.vector.quantize_mx(out=c[:].bitcast(FP8X4), scales=s[:], in_=dpi[b, g][:])
+            dpc[b, g] = (c, s)
+
+        ysall = keep.tile([128, ROWS], U8, name="ysall", align_bytes=64)
+        yt = {}
+
+        def stage2(b, t):
+            p = pp.tile([128, 512], F32, name="p")
+            for g in range(2):
+                c, s = dpc[b, g]
+                nc.tensor.matmul_mx(p[:], lhsT=wtc[:, g, 128 * t:128 * t + 128].bitcast(FP8X4), lhsT_scale=wts[:, g, 128 * t:128 * t + 128],
+                                    rhs=c[:].bitcast(FP8X4), rhs_scale=s[:], start=(g == 0), stop=(g == 1))
+            if t == 0:
+                y = work.tile([128, 4, 512], F32, name="yt")
+                yt[b] = y
+            nc.scalar.activation(out=yt[b][:, t, :], in_=p[:], func=ACT.Identity, scale=gmc[:, t:t + 1])
+
+        yi = {}
+
+        def y_inter(b, eng):
+            t = work.tile([128, 2048], BF16, name="yi", align_bytes=64)
+            yi[b] = t
+            for k in range(2):
+                dst = t[:, 1024 * k:1024 * k + 1024].rearrange("p (r t) -> p r t", t=4)
+                src = yt[b][:, :, 256 * k:256 * k + 256].rearrange("p t r -> p r t")
+                if eng == "v":
+                    nc.vector.tensor_copy(out=dst, in_=src)
+                else:
+                    nc.gpsimd.tensor_scalar(out=dst, in0=src, scalar1=1.0, scalar2=0.0, op0=ALU.mult, op1=ALU.add)
+
+        def y_quant(b):
+            c = work.tile([128, 512], U32, name="yc", align_bytes=64)
+            nc.vector.quantize_mx(out=c[:].bitcast(FP8X4), scales=ysall[:, 512 * b:512 * b + 512], in_=yi[b][:])
+            nc.sync.dma_start(out=words_out[0, :, 2048 * b:2048 * b + 2048].bitcast(I32), in_=c[:].bitcast(I32))
+            if b % 2 == 1:
+                c0 = 512 * (b - 1)
+                for q in range(4):
+                    nc.sync.dma_start(out=out_2[0, 4 * q:4 * q + 4, c0:c0 + 1024].bitcast(I32), in_=ysall[32 * q:32 * q + 4, c0:c0 + 1024].bitcast(I32))
+
+        yo = {}
+
+        def y_turn(b, k):
+            t = pt.tile([128, 4, 128], F32, name="tp")
+            for j in range(4):
+                nc.tensor.transpose(t[:, j, :], yt[b][:, j, 128 * k:128 * k + 128], identf[:])
+            ttile["y", b, k] = t
+
+        def y_out(b, k, eng):
+            if k % 2 == 0:
+                o = work.tile([128, 2, D], F32, name="yo", bufs=3)
+                yo[b, k // 2] = o
+            o = yo[b, k // 2]
+            dst = o[:, k % 2, :].rearrange("p (m t) -> p m t", t=4)
+            src = ttile["y", b, k][:].rearrange("p t m -> p m t")
+            if eng == "v":
+                nc.vector.tensor_copy(out=dst, in_=src)
+            else:
+                nc.scalar.copy(out=dst, in_=src)
+            if k % 2 == 1:
+                r0 = 512 * b + 128 * (k - 1)
+                nc.sync.dma_start(out=yr[r0:r0 + 256, :].rearrange("(k p) d -> p k d", p=128), in_=o[:])
+
+        beside = {}
+
+        def at(i, fn, *a):
+            beside.setdefault(i, []).append((fn, a))
+
+        for b, s0 in zip((1, 2, 3), X_AT):
+            at(s0, x_mul, b, 0)
+            at(s0 + 1, x_turn, b, 0)
+            at(s0 + 1, x_mul, b, 1)
+            at(s0 + 3, x_copy, b, 0, "v")
+            at(s0 + 3, x_turn, b, 1)
+            at(s0 + 5, x_copy, b, 1, "v")
+            at(s0 + 6, x_quant, b)
+        at(12, consts)
+        for b in (0, 1):
+            for k in range(4):
+                at(16 * b + 4 * k + 5, q_op, b, k)
+                at(16 * b + 4 * k + 6, n_op, b, k)
+        for k in range(4):
+            at(40 + 2 * k + 2, n_op, 2, 3 - k)
+            at(56 + 2 * k + 2, n_gps if N3_GPS else n_op, 3, 3 - k)
+        for i, (g, half) in enumerate(((0, 0), (0, 1), (1, 0), (1, 1))):
+            at(WT_AT + 2 * i, wt_turn, g, half)
+            at(WT_AT + 1 + 2 * i, wt_copy, g, half)
+            if half == 1:
+                at(WT_AT + 2 + 2 * i, wt_quant, g)
+        for a0, fn in zip(PAIR_AT, (pair1, pair2, pair3, pair4, pair5, pair6)):
+            at(a0, fn, 0)
+        for a0, fn in zip(PAIRB_AT, (pair1, pair2, pair3, pair4, pair5, pair6)):
+            at(a0, fn, 1)
+
+        def unit(i):
+            b, g, k = units[i]
+            dp_op(i)
+            if k is None or k == 3:
+                dp_quant(b, g)
+            if i + 2 < 16 or i >= 16:
+                delta_c(i + 2)
+
+        for i in range(len(units)):
+            at(U_AT[i], unit, i)
+        at(U_AT[0] - 1, delta_c, 0)
+        at(U_AT[0] - 1, delta_c, 1)
+        at(U_AT[16] - 1, delta_c, 16)
+        at(U_AT[16] - 1, delta_c, 17)
+        for bg, a0 in MP_AT:
+            at(a0, m_prime, *bg)
+        for b in range(NB):
+            a0 = L_AT[b]
+            for t in range(4):
+                at(a0 + t, stage2, b, t)
+            at(a0 + 5, y_inter, b, YI[b])
+            at(a0 + 9, y_quant, b)
+            for k in range(4):
+                at(a0 + 4 + k, y_turn, b, k)
+                at(a0 + 4 + k, y_out, b, k, "s")
+
+        s_list = []
+        for b in range(NB):
+            for k in range(4):
+                for ft in range(8):
+                    s_list.append((b, k, ft))
+        s_ready = {0: 15, 1: 31, 2: 47, 3: 55}
+        s_next = 0
+        n_mm = 0
+        for i in range(-1, max(beside) + 1):
+            if 0 <= i < len(acts):
+                act(i)
+            while n_mm < len(tiles) and (n_mm < PBUF or tiles[n_mm - PBUF][2] <= i):
+                stage1(n_mm)
+                n_mm += 1
+            if i < 0:
+                continue
+            for r in range(4 if i >= 31 else 3):
+                if s_next < len(s_list) and i >= s_ready[s_list[s_next][0]]:
+                    s_mm(*s_list[s_next])
+                    s_next += 1
+            for fn, a in beside.get(i, []):
+                fn(*a)

@@ -21,14 +21,20 @@ MPRIME = ((2, 1), (3, 0), (3, 1))
 PBUF = 3
 QBUF = 6
 N3_GPS = False
+HWBUF = 9
+PBUF = 3
+QBUF = 6
 YI = ("g", "g", "g", "v")
 MP_AT = [((2, 1), 64), ((3, 0), 70), ((3, 1), 74)]
-PAIR_AT = (39, 39, 39, 42, 44, 46)
-PAIRB_AT = (65, 67, 67, 70, 72, 74)
+SW_AT = ([2 * f + 1 for f in range(8)], [16 + f for f in range(8)], [47 - f for f in range(8)], [48 + f for f in range(8)])
+ST_AT = (17, 25, 49, 57)
+PAIR_AT = (27, 28, 30, 39, 41, 42, 44)
+PAIRB_AT = (59, 60, 62, 64, 66, 68, 70)
 WT_AT = 33
-X_AT = (1, 10, 22)
-U_AT = [48 + i for i in range(16)] + [78 + i for i in range(4)] + [83, 86, 89]
-L_AT = (65, 74, 86, 92)
+X_AT = (1, 10, 24)
+U_AT = [46 + i for i in range(16)] + [74 + i for i in range(4)] + [79, 82, 85]
+L_AT = (65, 73, 82, 88)
+
 
 def tile_smoothedrankdcginputgradient_kernel(tc, x, gamma, w1, g1, w2, gain, out_0, out_1, out_2):
     nc = tc.nc
@@ -44,7 +50,7 @@ def tile_smoothedrankdcginputgradient_kernel(tc, x, gamma, w1, g1, w2, gain, out
         pt = ctx.enter_context(tc.psum_pool(name="pt", bufs=2))
         pc = ctx.enter_context(tc.psum_pool(name="pc", bufs=2))
         ps = ctx.enter_context(tc.psum_pool(name="ps", bufs=1))
-        ctx.enter_context(tc.manual_schedule())
+        ctx.enter_context(tc.manual_schedule(engines={mybir.EngineType.Activation}))
 
         gz = keep.tile([128, D], BF16, name="gz")
         nc.vector.memset(gz[:], 0.0)
@@ -54,7 +60,7 @@ def tile_smoothedrankdcginputgradient_kernel(tc, x, gamma, w1, g1, w2, gain, out
         w1raw = keep.tile([128, 4, F], BF16, name="w1raw")
         xb = []
         for b in range(NB):
-            xt = keep.tile([128, 4, D], BF16, name="xb%d" % b)
+            xt = work.tile([128, 4, D], BF16, name="xt", tag="io", bufs=4)
             xb.append(xt)
 
         def load_x(b, half):
@@ -103,19 +109,6 @@ def tile_smoothedrankdcginputgradient_kernel(tc, x, gamma, w1, g1, w2, gain, out
         orow = keep.tile([128, 128], BF16, name="orow")
         nc.gpsimd.memset(orow[:], 0.0)
         nc.gpsimd.memset(orow[0:32, :], 1.0)
-        c_f = work.tile([64, F], F32, name="c_f", tag="yt")
-        nc.gpsimd.tensor_tensor(out=c_f[:], in0=g1r[:], in1=w2r[:], op=ALU.mult)
-        c_hi = work.tile([64, F], BF16, name="c_hi", tag="yt")
-        nc.gpsimd.tensor_scalar(out=c_hi[:], in0=c_f[:], scalar1=1.0, scalar2=0.0, op0=ALU.mult, op1=ALU.add)
-        c_lo = work.tile([64, F], BF16, name="c_lo", tag="dpi", align_bytes=64)
-        nc.gpsimd.tensor_tensor(out=c_lo[:], in0=c_f[:], in1=c_hi[:], op=ALU.subtract)
-        for g in range(2):
-            for r0, src in ((0, c_hi), (32, c_lo)):
-                nc.gpsimd.tensor_scalar(
-                    out=crow[r0:r0 + 32, 4 * g:4 * g + 4, :],
-                    in0=src[r0:r0 + 32, 512 * g:512 * g + 512].rearrange("k (m t) -> k t m", t=4),
-                    scalar1=1.0, scalar2=0.0, op0=ALU.mult, op1=ALU.add)
-
         warm = keep.tile([128, 1], F32, name="warm")
         nc.scalar.activation(out=warm[:], in_=ones[:, 0:1], func=ACT.Silu)
 
@@ -234,11 +227,28 @@ def tile_smoothedrankdcginputgradient_kernel(tc, x, gamma, w1, g1, w2, gain, out
             nc.tensor.transpose(t[:], gainz[:], identb[:])
             nc.vector.tensor_copy(out=gainc[:], in_=t[:, 0:16])
 
+        def c_rows():
+            c_f = work.tile([64, F], F32, name="c_f", tag="yt")
+            nc.vector.tensor_tensor(out=c_f[:], in0=g1r[:], in1=w2r[:], op=ALU.mult)
+            c_hi = work.tile([64, F], BF16, name="c_hi", tag="yt")
+            nc.vector.tensor_scalar(out=c_hi[:], in0=c_f[:], scalar1=1.0, scalar2=0.0, op0=ALU.mult, op1=ALU.add)
+            c_lo = work.tile([64, F], BF16, name="c_lo", tag="dpi", align_bytes=64)
+            nc.vector.tensor_tensor(out=c_lo[:], in0=c_f[:], in1=c_hi[:], op=ALU.subtract)
+            for g in range(2):
+                for r0, src in ((0, c_hi), (32, c_lo)):
+                    nc.vector.tensor_scalar(
+                        out=crow[r0:r0 + 32, 4 * g:4 * g + 4, :],
+                        in0=src[r0:r0 + 32, 512 * g:512 * g + 512].rearrange("k (m t) -> k t m", t=4),
+                        scalar1=1.0, scalar2=0.0, op0=ALU.mult, op1=ALU.add)
+
         acts = []
-        for b in (0, 1):
-            for ft in range(8):
-                acts.append(("silu", b, ft))
-                acts.append(("tanh", b, ft))
+        for ft in range(8):
+            acts.append(("silu", 0, ft))
+            acts.append(("tanh", 0, ft))
+        for ft in range(8):
+            acts.append(("silu", 1, ft))
+        for ft in range(7, -1, -1):
+            acts.append(("tanh", 1, ft))
         for ft in range(8):
             acts.append(("sig", 2, ft))
         for ft in range(7, -1, -1):
@@ -250,7 +260,7 @@ def tile_smoothedrankdcginputgradient_kernel(tc, x, gamma, w1, g1, w2, gain, out
         tiles = []
         where = {}
         for i, (kind, b, ft) in enumerate(acts):
-            kept = b < 2 or ft >= 8 - PBUF
+            kept = b == 0 or ft >= 8 - PBUF
             if (b, ft) in where and kept:
                 m = where[b, ft]
                 tiles[m] = (b, ft, i)
@@ -308,15 +318,29 @@ def tile_smoothedrankdcginputgradient_kernel(tc, x, gamma, w1, g1, w2, gain, out
 
         sps = {}
 
-        def s_mm(b, k, ft):
-            h = b // 2
-            if b % 2 == 0 and k == 0 and ft == 0:
-                t = ps.tile([128, 8], F32, name="sp")
-                sps[h] = t
+        hw = {}
+
+        def s_weigh(b, ft):
             g, t = divmod(ft, 4)
-            j = 4 * (b % 2) + k
-            nc.tensor.matmul(sps[h][:, j:j + 1], lhsT=hn[b, g][:, t, 128 * k:128 * k + 128], rhs=w2c[:, ft:ft + 1],
-                             start=(ft == 0), stop=(ft == 7))
+            w_t = work.tile([128, 512], F32, name="hw", bufs=HWBUF)
+            nc.gpsimd.tensor_scalar(out=w_t[:], in0=hn[b, g][:, t, :], scalar1=w2c[:, ft:ft + 1], scalar2=0.0, op0=ALU.mult, op1=ALU.add)
+            hw[b, ft] = w_t
+
+        def s_turn(b):
+            t = ps.tile([128, 4, 128], F32, name="sp")
+            for k in range(4):
+                for ft in range(8):
+                    nc.tensor.matmul(t[:, k, :], lhsT=hw[b, ft][:, 128 * k:128 * k + 128], rhs=identf[:], start=(ft == 0), stop=(ft == 7), is_transpose=True)
+            sps[b] = t
+
+        s_col = {}
+
+        def s_sum(b):
+            h = b // 2
+            if h not in s_col:
+                s_t = pairp.tile([128, 8], F32, name="s")
+                s_col[h] = s_t
+            nc.vector.tensor_reduce(out=s_col[h][:, 4 * (b % 2):4 * (b % 2) + 4], in_=sps[b][:], axis=AX.X, op=ALU.add)
 
         st = {}
 
@@ -331,8 +355,7 @@ def tile_smoothedrankdcginputgradient_kernel(tc, x, gamma, w1, g1, w2, gain, out
             return bank
 
         def pair1(h):
-            s = pairp.tile([128, 8], F32, name="s")
-            nc.vector.tensor_copy(out=s[:], in_=sps[h][:])
+            s = s_col[h]
             se = pairp.tile([128, 8, 32], F32, name="se")
             nc.vector.tensor_tensor(out=se[:], in0=bc(s[:]), in1=ecol[:].unsqueeze(1).to_broadcast([128, 8, 32]), op=ALU.mult)
             r = ps.tile([128, 256], F32, name="sp")
@@ -350,19 +373,22 @@ def tile_smoothedrankdcginputgradient_kernel(tc, x, gamma, w1, g1, w2, gain, out
             d["kk"] = kk
             d["kn"] = kn
 
-        def pair3(h):
+        def pair3a(h):
             d = st[h]
             u = pairp.tile([128, 8], F32, name="u")
             nc.vector.tensor_reduce(out=u[:], in_=d["kk"][:], axis=AX.X, op=ALU.add)
             u2 = pairp.tile([128, 8], F32, name="u2")
             nc.vector.tensor_scalar_add(out=u2[:], in0=u[:], scalar1=1.5)
-            ln = pairp.tile([128, 8], F32, name="ln")
-            nc.scalar.activation(out=ln[:], in_=u2[:], func=ACT.Ln)
             kp = pairp.tile([128, 8, 32], F32, name="kp")
             nc.vector.tensor_tensor(out=kp[:], in0=d["kk"][:], in1=d["kn"][:], op=ALU.mult)
             d["u2"] = u2
-            d["ln"] = ln
             d["kp"] = kp
+
+        def pair3(h):
+            d = st[h]
+            ln = pairp.tile([128, 8], F32, name="ln")
+            nc.scalar.activation(out=ln[:], in_=d["u2"][:], func=ACT.Ln)
+            d["ln"] = ln
 
         def pair4(h):
             d = st[h]
@@ -510,7 +536,7 @@ def tile_smoothedrankdcginputgradient_kernel(tc, x, gamma, w1, g1, w2, gain, out
 
         def y_out(b, k, eng):
             if k % 2 == 0:
-                o = work.tile([128, 2, D], F32, name="yo", bufs=3)
+                o = work.tile([128, 2, D], F32, name="yo", tag="io", bufs=4)
                 yo[b, k // 2] = o
             o = yo[b, k // 2]
             dst = o[:, k % 2, :].rearrange("p (m t) -> p m t", t=4)
@@ -537,10 +563,12 @@ def tile_smoothedrankdcginputgradient_kernel(tc, x, gamma, w1, g1, w2, gain, out
             at(s0 + 5, x_copy, b, 1, "v")
             at(s0 + 6, x_quant, b)
         at(12, consts)
-        for b in (0, 1):
-            for k in range(4):
-                at(16 * b + 4 * k + 5, q_op, b, k)
-                at(16 * b + 4 * k + 6, n_op, b, k)
+        at(2, c_rows)
+        for k in range(4):
+            at(4 * k + 5, q_op, 0, k)
+            at(4 * k + 6, n_op, 0, k)
+            at(26 + 2 * k, q_op, 1, 3 - k)
+            at(27 + 2 * k, n_op, 1, 3 - k)
         for k in range(4):
             at(40 + 2 * k + 2, n_op, 2, 3 - k)
             at(56 + 2 * k + 2, n_gps if N3_GPS else n_op, 3, 3 - k)
@@ -549,9 +577,9 @@ def tile_smoothedrankdcginputgradient_kernel(tc, x, gamma, w1, g1, w2, gain, out
             at(WT_AT + 1 + 2 * i, wt_copy, g, half)
             if half == 1:
                 at(WT_AT + 2 + 2 * i, wt_quant, g)
-        for a0, fn in zip(PAIR_AT, (pair1, pair2, pair3, pair4, pair5, pair6)):
+        for a0, fn in zip(PAIR_AT, (pair1, pair2, pair3a, pair3, pair4, pair5, pair6)):
             at(a0, fn, 0)
-        for a0, fn in zip(PAIRB_AT, (pair1, pair2, pair3, pair4, pair5, pair6)):
+        for a0, fn in zip(PAIRB_AT, (pair1, pair2, pair3a, pair3, pair4, pair5, pair6)):
             at(a0, fn, 1)
 
         def unit(i):
@@ -580,13 +608,11 @@ def tile_smoothedrankdcginputgradient_kernel(tc, x, gamma, w1, g1, w2, gain, out
                 at(a0 + 4 + k, y_turn, b, k)
                 at(a0 + 4 + k, y_out, b, k, "s")
 
-        s_list = []
         for b in range(NB):
-            for k in range(4):
-                for ft in range(8):
-                    s_list.append((b, k, ft))
-        s_ready = {0: 15, 1: 31, 2: 47, 3: 55}
-        s_next = 0
+            for ft in range(8):
+                at(SW_AT[b][ft], s_weigh, b, ft)
+            at(ST_AT[b], s_turn, b)
+            at(ST_AT[b] + 1, s_sum, b)
         n_mm = 0
         for i in range(-1, max(beside) + 1):
             if 0 <= i < len(acts):
@@ -596,9 +622,5 @@ def tile_smoothedrankdcginputgradient_kernel(tc, x, gamma, w1, g1, w2, gain, out
                 n_mm += 1
             if i < 0:
                 continue
-            for r in range(4 if i >= 31 else 3):
-                if s_next < len(s_list) and i >= s_ready[s_list[s_next][0]]:
-                    s_mm(*s_list[s_next])
-                    s_next += 1
             for fn, a in beside.get(i, []):
                 fn(*a)

@@ -17,23 +17,38 @@ AX = mybir.AxisListType
 ROWS, D, F = 2048, 512, 1024
 FLOPS = 4 * ROWS * D * F
 NB = 4
+BORD = (0, 1, 2, 3)
+SWEEPS = (("mix", 0, 1), ("silu", 1, 1), ("sig", 1, -1), ("mix", 2, 1), ("silu", 3, 1), ("sig", 3, -1))
+GROUPS = ((0, 1), (2, 3))
 MPRIME = ((2, 1), (3, 0), (3, 1))
-PBUF = 3
-QBUF = 6
-N3_GPS = False
+MP_ENG = "sss"
+WEIGH = "vvvvsvgv"
 HWBUF = 9
 PBUF = 3
-QBUF = 6
-YI = ("g", "g", "g", "v")
-MP_AT = [((2, 1), 64), ((3, 0), 70), ((3, 1), 74)]
-SW_AT = ([2 * f + 1 for f in range(8)], [16 + f for f in range(8)], [47 - f for f in range(8)], [48 + f for f in range(8)])
-ST_AT = (17, 25, 49, 57)
-PAIR_AT = (27, 28, 30, 39, 41, 42, 44)
-PAIRB_AT = (59, 60, 62, 64, 66, 68, 70)
-WT_AT = 33
-X_AT = (1, 10, 24)
-U_AT = [46 + i for i in range(16)] + [74 + i for i in range(4)] + [79, 82, 85]
-L_AT = (65, 73, 82, 88)
+QBUF = 5
+ILBUF = 5
+CHUNK = (4, 4, 4, 2)
+YI = "sssg"
+SS = (1, 0, 1, 0)
+ST_D = (3, 1, 3, 4)
+N_D = (11, 9, 13, 18)
+W_D = 1
+L_P = (1, 7, 26, 31)
+L_D = (2, 4, 6, 5)
+YO = ("vsss", "ssss", "sssv", "sssv")
+ID = ("ssss", "ssss", "ssss", "vvvs")
+WI = "svgsvsss"
+LO = "xywv"
+NE = ("vvvv", "vvvv", "vvvv", "vvvv")
+KP = "v"
+WC = "vvvs"
+MP_AT = (67, 84, 91)
+PAIR_AT = ((31, 31, 31), (61, 62, 62))
+CR_AT = 6
+WT_AT = (41, 46, 48, 53)
+X_AT = (7, 10, 29)
+XD = 0
+U_AT = (57, 68, 86, 80)
 
 
 def tile_smoothedrankdcginputgradient_kernel(tc, x, gamma, w1, g1, w2, gain, out_0, out_1, out_2):
@@ -52,11 +67,8 @@ def tile_smoothedrankdcginputgradient_kernel(tc, x, gamma, w1, g1, w2, gain, out
         ps = ctx.enter_context(tc.psum_pool(name="ps", bufs=1))
         ctx.enter_context(tc.manual_schedule(engines={mybir.EngineType.Activation}))
 
-        gz = keep.tile([128, D], BF16, name="gz")
-        nc.vector.memset(gz[:], 0.0)
         ones = keep.tile([128, 128], BF16, name="ones")
         nc.vector.memset(ones[:], 1.0)
-        nc.scalar.dma_start(out=gz[0:1, :], in_=gamma.unsqueeze(0))
         w1raw = keep.tile([128, 4, F], BF16, name="w1raw")
         xb = []
         for b in range(NB):
@@ -70,16 +82,17 @@ def tile_smoothedrankdcginputgradient_kernel(tc, x, gamma, w1, g1, w2, gain, out
         def load_w(g):
             nc.sync.dma_start(out=w1raw[:, :, 512 * g:512 * g + 512], in_=w1[:, 512 * g:512 * g + 512].rearrange("(p j) f -> p j f", j=4))
 
-        load_x(0, 0)
-        load_w(0)
-        load_x(0, 1)
-        load_w(1)
+        for what in LO:
+            if what in "xy":
+                load_x(0, "xy".index(what))
+            else:
+                load_w("wv".index(what))
+        gmb = keep.tile([128, 4], BF16, name="gmb")
+        nc.scalar.dma_start(out=gmb[:], in_=gamma.rearrange("(p t) -> p t", t=4))
         g1b = keep.tile([128, 2, 4], BF16, name="g1b")
         nc.scalar.dma_start(out=g1b[:], in_=g1.rearrange("(g p t) -> p g t", g=2, t=4))
         w2b = keep.tile([128, 2, 4], BF16, name="w2b")
         nc.scalar.dma_start(out=w2b[:], in_=w2.rearrange("(g p t) -> p g t", g=2, t=4))
-        gmb = keep.tile([128, 4], BF16, name="gmb")
-        nc.scalar.dma_start(out=gmb[:], in_=gamma.rearrange("(p t) -> p t", t=4))
         for b in (1, 2, 3):
             load_x(b, 0)
             load_x(b, 1)
@@ -95,27 +108,16 @@ def tile_smoothedrankdcginputgradient_kernel(tc, x, gamma, w1, g1, w2, gain, out
         identb = keep.tile([128, 128], BF16, name="identb")
         nc.gpsimd.tensor_scalar(out=identb[:], in0=identf[:], scalar1=1.0, scalar2=0.0, op0=ALU.mult, op1=ALU.add)
         nc.sync.dma_start(out=gainz[0:16, :], in_=gain.rearrange("(a q) n -> a (q n)", q=4))
-        g1r = work.tile([64, F], BF16, name="g1r", tag="yi", align_bytes=64)
-        w2r = work.tile([64, F], BF16, name="w2r", tag="yi", align_bytes=64)
-        nc.gpsimd.memset(g1r[:], 0.0)
-        nc.gpsimd.memset(w2r[:], 0.0)
-        for r0 in (0, 32):
-            nc.sync.dma_start(out=g1r[r0:r0 + 3, :], in_=g1.partition_broadcast(3))
-            nc.sync.dma_start(out=w2r[r0:r0 + 3, :], in_=w2.partition_broadcast(3))
         crow = keep.tile([128, 8, 128], BF16, name="crow")
-        nc.gpsimd.memset(crow[:], 0.0)
+        cparts = keep.tile([128, 8, 128], BF16, name="cparts")
+        nc.gpsimd.memset(cparts[:], 0.0)
         dparts = keep.tile([128, 16, 128], BF16, name="dparts")
         nc.gpsimd.memset(dparts[:], 0.0)
         orow = keep.tile([128, 128], BF16, name="orow")
         nc.gpsimd.memset(orow[:], 0.0)
         nc.gpsimd.memset(orow[0:32, :], 1.0)
         warm = keep.tile([128, 1], F32, name="warm")
-        nc.scalar.activation(out=warm[:], in_=ones[:, 0:1], func=ACT.Silu)
-
-        gps = pt.tile([128, D], F32, name="tp")
-        nc.tensor.matmul(gps[:], lhsT=ones[:], rhs=gz[:], start=True, stop=True)
-        gbc = keep.tile([128, D], BF16, name="gbc")
-        nc.vector.tensor_copy(out=gbc[:], in_=gps[:])
+        nc.scalar.activation(out=warm[:], in_=ones[:, 0:1], func=ACT.Sigmoid if SWEEPS[0][0] == "sig" else ACT.Silu)
 
         w1c = keep.tile([128, 2, 512], U32, name="w1c", align_bytes=64)
         w1s = keep.tile([128, 2, 512], U8, name="w1s", align_bytes=64)
@@ -128,50 +130,46 @@ def tile_smoothedrankdcginputgradient_kernel(tc, x, gamma, w1, g1, w2, gain, out
             t2 = keep.tile([128, 512], U8, name="xs%d" % b, align_bytes=64)
             xc.append(t1)
             xs.append(t2)
+        done = set()
         xg = {}
         xi = {}
         ttile = {}
 
-        def x_mul(b, half):
-            t = work.tile([128, 2, D], BF16, name="xg")
-            nc.vector.tensor_tensor(out=t[:], in0=xb[b][:, 2 * half:2 * half + 2, :],
-                                    in1=gbc[:].unsqueeze(1).to_broadcast([128, 2, D]), op=ALU.mult)
-            xg[b, half] = t
-
         def x_turn(b, half):
-            t = pt.tile([128, 2, 2, 128], F32, name="tp")
-            words = xg[b, half][:].bitcast(F32)
+            t = pt.tile([128, 2, 256], F32, name="tp")
+            words = xb[b][:, 2 * half:2 * half + 2, :].bitcast(F32)
             for k in range(2):
                 for u in range(2):
-                    nc.tensor.transpose(t[:, k, u, :], words[:, k, u:256:2], identf[:])
+                    nc.tensor.transpose(t[:, u, 128 * k:128 * k + 128], words[:, k, u:256:2], identf[:])
             ttile[b, half] = t
 
-        def x_copy(b, half, eng):
+        def x_copy(b, half):
             if half == 0:
-                t = work.tile([128, 2048], BF16, name="xi", align_bytes=64)
+                t = work.tile([128, 2048], BF16, name="xi", tag="il", bufs=ILBUF, align_bytes=64)
                 xi[b] = t
-            dst = xi[b][:, 1024 * half:1024 * half + 1024].bitcast(F32).rearrange("p (k r u) -> p k r u", k=2, u=2)
-            src = ttile[b, half][:].rearrange("p k u r -> p k r u")
-            if eng == "v":
-                nc.vector.tensor_copy(out=dst, in_=src)
-            else:
-                nc.scalar.copy(out=dst, in_=src)
+            dst = xi[b][:, 1024 * half:1024 * half + 1024].rearrange("p (r u e) -> p r u e", u=2, e=2)
+            src = ttile[b, half][:].bitcast(BF16).rearrange("p u (r e) -> p r u e", e=2)
+            gam = gmb[:].rearrange("p (u e) -> p u e", e=2).unsqueeze(1).to_broadcast([128, 256, 2, 2])
+            nc.vector.tensor_tensor(out=dst, in0=src, in1=gam, op=ALU.mult)
 
         def x_quant(b):
             nc.vector.quantize_mx(out=xc[b][:].bitcast(FP8X4), scales=xs[b][:], in_=xi[b][:])
 
         wi = {}
 
-        def w_inter(g, eng):
-            t = work.tile([128, 2048], BF16, name="wi", align_bytes=64)
+        def w_inter(g):
+            t = work.tile([128, 2048], BF16, name="wi", tag="il", bufs=ILBUF, align_bytes=64)
             wi[g] = t
             dst = t[:].rearrange("p (t m j) -> p t m j", t=4, j=4)
             src = w1raw[:, :, 512 * g:512 * g + 512].rearrange("p j (m t) -> p t m j", t=4)
             for t2 in range(4):
+                eng = WI[4 * g + t2]
                 if eng == "v":
                     nc.vector.tensor_copy(out=dst[:, t2, :, :], in_=src[:, t2, :, :])
-                else:
+                elif eng == "s":
                     nc.scalar.copy(out=dst[:, t2, :, :], in_=src[:, t2, :, :])
+                else:
+                    nc.gpsimd.tensor_scalar(out=dst[:, t2, :, :], in0=src[:, t2, :, :], scalar1=1.0, scalar2=0.0, op0=ALU.mult, op1=ALU.add)
 
         def w_quant(g):
             nc.vector.quantize_mx(out=w1c[:, g, :].bitcast(FP8X4), scales=w1s[:, g, :], in_=wi[g][:])
@@ -184,26 +182,28 @@ def tile_smoothedrankdcginputgradient_kernel(tc, x, gamma, w1, g1, w2, gain, out
                     nc.tensor.transpose(t[:, k, u, :], words[:, 256 * g + u:256 * g + 256:2], identf[:])
             ttile["w", g, half] = t
 
-        def wt_copy(g, half):
+        def wt_copy(g, half, eng):
             if half == 0:
-                t = work.tile([128, 2048], BF16, name="wi", align_bytes=64)
+                t = work.tile([128, 2048], BF16, name="wi", tag="il", bufs=ILBUF, align_bytes=64)
                 wi["t", g] = t
             dst = wi["t", g][:, 1024 * half:1024 * half + 1024].bitcast(F32).rearrange("p (k m u) -> p k m u", k=2, u=2)
-            nc.vector.tensor_copy(out=dst, in_=ttile["w", g, half][:].rearrange("p k u m -> p k m u"))
+            src = ttile["w", g, half][:].rearrange("p k u m -> p k m u")
+            if eng == "v":
+                nc.vector.tensor_copy(out=dst, in_=src)
+            else:
+                nc.scalar.copy(out=dst, in_=src)
 
         def wt_quant(g):
             nc.vector.quantize_mx(out=wtc[:, g, :].bitcast(FP8X4), scales=wts[:, g, :], in_=wi["t", g][:])
 
-        x_mul(0, 0)
-        w_inter(0, "v")
         x_turn(0, 0)
-        x_mul(0, 1)
-        w_quant(0)
-        x_copy(0, 0, "s")
+        x_copy(0, 0)
         x_turn(0, 1)
-        x_copy(0, 1, "v")
+        x_copy(0, 1)
+        w_inter(0)
         x_quant(0)
-        w_inter(1, "s")
+        w_quant(0)
+        w_inter(1)
         g1c = keep.tile([128, 8], F32, name="g1c")
         nc.vector.tensor_copy(out=g1c[:], in_=g1b[:].rearrange("p g t -> p (g t)"))
         ng1c = keep.tile([128, 8], F32, name="ng1c")
@@ -228,40 +228,29 @@ def tile_smoothedrankdcginputgradient_kernel(tc, x, gamma, w1, g1, w2, gain, out
             nc.vector.tensor_copy(out=gainc[:], in_=t[:, 0:16])
 
         def c_rows():
-            c_f = work.tile([64, F], F32, name="c_f", tag="yt")
-            nc.vector.tensor_tensor(out=c_f[:], in0=g1r[:], in1=w2r[:], op=ALU.mult)
-            c_hi = work.tile([64, F], BF16, name="c_hi", tag="yt")
-            nc.vector.tensor_scalar(out=c_hi[:], in0=c_f[:], scalar1=1.0, scalar2=0.0, op0=ALU.mult, op1=ALU.add)
-            c_lo = work.tile([64, F], BF16, name="c_lo", tag="dpi", align_bytes=64)
-            nc.vector.tensor_tensor(out=c_lo[:], in0=c_f[:], in1=c_hi[:], op=ALU.subtract)
-            for g in range(2):
-                for r0, src in ((0, c_hi), (32, c_lo)):
-                    nc.vector.tensor_scalar(
-                        out=crow[r0:r0 + 32, 4 * g:4 * g + 4, :],
-                        in0=src[r0:r0 + 32, 512 * g:512 * g + 512].rearrange("k (m t) -> k t m", t=4),
-                        scalar1=1.0, scalar2=0.0, op0=ALU.mult, op1=ALU.add)
+            c_hi = keep.tile([128, 8, 1], BF16, name="c_hi")
+            cv = c8[:].unsqueeze(2)
+            nc.vector.tensor_copy(out=c_hi[:], in_=cv)
+            nc.vector.tensor_copy(out=cparts[:, :, 0:3], in_=c_hi[:].to_broadcast([128, 8, 3]))
+            nc.vector.tensor_tensor(out=cparts[:, :, 32:35], in0=cv.to_broadcast([128, 8, 3]), in1=c_hi[:].to_broadcast([128, 8, 3]), op=ALU.subtract)
+            t = pt.tile([128, 8, 128], BF16, name="tp")
+            for j in range(8):
+                nc.tensor.transpose(t[:, j, :], cparts[:, j, :], identb[:])
+            nc.scalar.copy(out=crow[:], in_=t[:])
 
         acts = []
-        for ft in range(8):
-            acts.append(("silu", 0, ft))
-            acts.append(("tanh", 0, ft))
-        for ft in range(8):
-            acts.append(("silu", 1, ft))
-        for ft in range(7, -1, -1):
-            acts.append(("tanh", 1, ft))
-        for ft in range(8):
-            acts.append(("sig", 2, ft))
-        for ft in range(7, -1, -1):
-            acts.append(("silu", 2, ft))
-        for ft in range(8):
-            acts.append(("silu", 3, ft))
-        for ft in range(7, -1, -1):
-            acts.append(("sig", 3, ft))
+        for kind, b, order in SWEEPS:
+            for ft in range(8)[::order]:
+                if kind == "mix":
+                    acts.append(("silu", b, ft))
+                    acts.append(("tanh", b, ft))
+                else:
+                    acts.append((kind, b, ft))
         tiles = []
         where = {}
         for i, (kind, b, ft) in enumerate(acts):
-            kept = b == 0 or ft >= 8 - PBUF
-            if (b, ft) in where and kept:
+            kept = ft >= 8 - PBUF or (i and acts[i - 1][1:] == (b, ft))
+            if (b, ft) in where and kept and i - tiles[where[b, ft]][2] <= 2 * PBUF:
                 m = where[b, ft]
                 tiles[m] = (b, ft, i)
             else:
@@ -285,36 +274,34 @@ def tile_smoothedrankdcginputgradient_kernel(tc, x, gamma, w1, g1, w2, gain, out
             g, t = divmod(ft, 4)
             if kind == "silu":
                 if (b, g) not in hn:
-                    h_t = work.tile([128, 4, 512], F32, name="h", bufs=4)
+                    h_t = work.tile([128, 4, 512], F32, name="h", bufs=8)
                     hn[b, g] = h_t
                 nc.scalar.activation(out=hn[b, g][:, t, :], in_=acc[b, ft][:], func=ACT.Silu, scale=g1c[:, ft:ft + 1])
                 return
-            if (b, g) not in qn:
-                q = work.tile([128, 4, 512], F32, name="q", bufs=QBUF)
-                qn[b, g] = q
-            dst = qn[b, g][:, t, :]
+            if (b, ft // 2) not in qn:
+                q = work.tile([128, 2, 512], F32, name="q", bufs=QBUF)
+                qn[b, ft // 2] = q
+            dst = qn[b, ft // 2][:, ft % 2, :]
             if kind == "tanh":
                 nc.scalar.activation(out=dst, in_=acc[b, ft][:], func=ACT.Tanh, scale=hg1c[:, ft:ft + 1])
             else:
                 nc.scalar.activation(out=dst, in_=acc[b, ft][:], func=ACT.Sigmoid, scale=ng1c[:, ft:ft + 1])
 
         def q_op(b, k):
-            g, t = divmod(2 * k, 4)
-            q = qn[b, g][:, t:t + 2, :]
+            q = qn[b, k][:]
             nc.vector.tensor_scalar(out=q, in0=q, scalar1=-0.5, scalar2=0.5, op0=ALU.mult, op1=ALU.add)
+            done.add(("q", b, k))
 
         def n_op(b, k):
             g, t = divmod(2 * k, 4)
-            q = qn[b, g][:, t:t + 2, :]
-            nc.vector.scalar_tensor_tensor(out=q, in0=hn[b, g][:, t:t + 2, :], scalar=1.0, in1=q, op0=ALU.subtract, op1=ALU.mult)
-
-        def n_gps(b, k):
-            g, t = divmod(2 * k, 4)
-            for j in range(2):
-                q = qn[b, g][:, t + j, :]
-                h_t = hn[b, g][:, t + j, :]
-                nc.gpsimd.tensor_scalar(out=h_t, in0=h_t, scalar1=1.0, scalar2=-1.0, op0=ALU.mult, op1=ALU.add)
-                nc.gpsimd.tensor_tensor(out=q, in0=h_t, in1=q, op=ALU.mult)
+            hv = hn[b, g][:, t:t + 2, :]
+            assert ("w", b, 2 * k) in done and ("w", b, 2 * k + 1) in done
+            done.add(("n", b, k))
+            if NE[b][k] == "v":
+                nc.vector.scalar_tensor_tensor(out=hv, in0=hv, scalar=1.0, in1=qn[b, k][:], op0=ALU.subtract, op1=ALU.mult)
+            else:
+                nc.gpsimd.tensor_scalar(out=hv, in0=hv, scalar1=1.0, scalar2=-1.0, op0=ALU.mult, op1=ALU.add)
+                nc.gpsimd.tensor_tensor(out=hv, in0=hv, in1=qn[b, k][:], op=ALU.mult)
 
         sps = {}
 
@@ -323,139 +310,127 @@ def tile_smoothedrankdcginputgradient_kernel(tc, x, gamma, w1, g1, w2, gain, out
         def s_weigh(b, ft):
             g, t = divmod(ft, 4)
             w_t = work.tile([128, 512], F32, name="hw", bufs=HWBUF)
-            nc.gpsimd.tensor_scalar(out=w_t[:], in0=hn[b, g][:, t, :], scalar1=w2c[:, ft:ft + 1], scalar2=0.0, op0=ALU.mult, op1=ALU.add)
+            if WEIGH[ft] == "v":
+                nc.vector.tensor_scalar_mul(out=w_t[:], in0=hn[b, g][:, t, :], scalar1=w2c[:, ft:ft + 1])
+            elif WEIGH[ft] == "s":
+                nc.scalar.mul(out=w_t[:], in_=hn[b, g][:, t, :], mul=w2c[:, ft:ft + 1])
+            else:
+                nc.gpsimd.tensor_scalar(out=w_t[:], in0=hn[b, g][:, t, :], scalar1=w2c[:, ft:ft + 1], scalar2=0.0, op0=ALU.mult, op1=ALU.add)
             hw[b, ft] = w_t
+            done.add(("w", b, ft))
 
-        def s_turn(b):
-            t = ps.tile([128, 4, 128], F32, name="sp")
-            for k in range(4):
-                for ft in range(8):
-                    nc.tensor.matmul(t[:, k, :], lhsT=hw[b, ft][:, 128 * k:128 * k + 128], rhs=identf[:], start=(ft == 0), stop=(ft == 7), is_transpose=True)
-            sps[b] = t
+        def s_turn(b, k):
+            if k == 0:
+                t = ps.tile([128, 4, 128], F32, name="sp")
+                sps[b] = t
+            for ft in range(8):
+                nc.tensor.matmul(sps[b][:, k, :], lhsT=hw[b, ft][:, 128 * k:128 * k + 128], rhs=identf[:], start=(ft == 0), stop=(ft == 7), is_transpose=True)
 
-        s_col = {}
+        s_all = keep.tile([128, 16], F32, name="s_all")
 
         def s_sum(b):
-            h = b // 2
-            if h not in s_col:
-                s_t = pairp.tile([128, 8], F32, name="s")
-                s_col[h] = s_t
-            nc.vector.tensor_reduce(out=s_col[h][:, 4 * (b % 2):4 * (b % 2) + 4], in_=sps[b][:], axis=AX.X, op=ALU.add)
+            nc.vector.tensor_reduce(out=s_all[:, 4 * b:4 * b + 4], in_=sps[b][:], axis=AX.X, op=ALU.add)
+            done.add(("sum", b))
 
         st = {}
-
-        def bc(ap):
-            return ap.unsqueeze(2).to_broadcast([128, 8, 32])
-
-        def pair_bank(h, shape, dtype):
-            if h == 0:
-                bank = pc.tile(shape, dtype, name="c")
-            else:
-                bank = ps.tile(shape, dtype, name="sp")
-            return bank
+        dd = keep.tile([128, ROWS], BF16, name="dd")
 
         def pair1(h):
-            s = s_col[h]
-            se = pairp.tile([128, 8, 32], F32, name="se")
-            nc.vector.tensor_tensor(out=se[:], in0=bc(s[:]), in1=ecol[:].unsqueeze(1).to_broadcast([128, 8, 32]), op=ALU.mult)
-            r = ps.tile([128, 256], F32, name="sp")
+            lo, n = 4 * GROUPS[h][0], 4 * len(GROUPS[h])
+            assert all(("sum", b) in done for b in GROUPS[h])
+            s = s_all[:, lo:lo + n]
+            se = pairp.tile([128, n, 32], F32, name="se")
+            nc.vector.tensor_tensor(out=se[:], in0=s.unsqueeze(2).to_broadcast([128, n, 32]), in1=ecol[:].unsqueeze(1).to_broadcast([128, n, 32]), op=ALU.mult)
+            r = ps.tile([128, 32 * n], F32, name="sp")
             nc.tensor.matmul(r[:], lhsT=blk[:], rhs=se[:].rearrange("p a i -> p (a i)"), start=True, stop=True)
-            st[h] = {"s": s, "r": r}
+            df = pairp.tile([128, n, 32], F32, name="df")
+            nc.vector.tensor_tensor(out=df[:], in0=r[:].rearrange("p (a i) -> p a i", i=32), in1=s.unsqueeze(2).to_broadcast([128, n, 32]), op=ALU.subtract)
+            st[h] = {"df": df, "n": n, "lo": lo}
 
         def pair2(h):
             d = st[h]
-            df = pairp.tile([128, 8, 32], F32, name="df")
-            nc.vector.tensor_tensor(out=df[:], in0=d["r"][:].rearrange("p (a i) -> p a i", i=32), in1=bc(d["s"][:]), op=ALU.subtract)
-            kk = pairp.tile([128, 8, 32], F32, name="kk")
-            nc.scalar.activation(out=kk[:], in_=df[:], func=ACT.Sigmoid, scale=2.0)
-            kn = pairp.tile([128, 8, 32], F32, name="kn")
-            nc.scalar.activation(out=kn[:], in_=df[:], func=ACT.Sigmoid, scale=-2.0)
-            d["kk"] = kk
-            d["kn"] = kn
-
-        def pair3a(h):
-            d = st[h]
-            u = pairp.tile([128, 8], F32, name="u")
-            nc.vector.tensor_reduce(out=u[:], in_=d["kk"][:], axis=AX.X, op=ALU.add)
-            u2 = pairp.tile([128, 8], F32, name="u2")
+            kk = pairp.tile([128, d["n"], 32], F32, name="kk")
+            nc.scalar.activation(out=kk[:], in_=d["df"][:], func=ACT.Sigmoid, scale=2.0)
+            kn = pairp.tile([128, d["n"], 32], F32, name="kn")
+            nc.scalar.activation(out=kn[:], in_=d["df"][:], func=ACT.Sigmoid, scale=-2.0)
+            u = pairp.tile([128, d["n"]], F32, name="u")
+            nc.vector.tensor_reduce(out=u[:], in_=kk[:], axis=AX.X, op=ALU.add)
+            u2 = pairp.tile([128, d["n"]], F32, name="u2")
             nc.vector.tensor_scalar_add(out=u2[:], in0=u[:], scalar1=1.5)
-            kp = pairp.tile([128, 8, 32], F32, name="kp")
-            nc.vector.tensor_tensor(out=kp[:], in0=d["kk"][:], in1=d["kn"][:], op=ALU.mult)
+            kp = pairp.tile([128, d["n"], 32], F32, name="kp")
+            eng = nc.vector if KP == "v" else nc.gpsimd
+            eng.tensor_tensor(out=kp[:], in0=kk[:], in1=kn[:], op=ALU.mult)
             d["u2"] = u2
             d["kp"] = kp
 
         def pair3(h):
             d = st[h]
-            ln = pairp.tile([128, 8], F32, name="ln")
+            n, lo = d["n"], d["lo"]
+            ln = pairp.tile([128, n], F32, name="ln")
             nc.scalar.activation(out=ln[:], in_=d["u2"][:], func=ACT.Ln)
-            d["ln"] = ln
-
-        def pair4(h):
-            d = st[h]
-            t1 = pairp.tile([128, 8], F32, name="t1")
-            nc.vector.tensor_tensor(out=t1[:], in0=d["ln"][:], in1=d["ln"][:], op=ALU.mult)
-            t2 = pairp.tile([128, 8], F32, name="t2")
+            t1 = pairp.tile([128, n], F32, name="t1")
+            nc.vector.tensor_tensor(out=t1[:], in0=ln[:], in1=ln[:], op=ALU.mult)
+            t2 = pairp.tile([128, n], F32, name="t2")
             nc.vector.tensor_tensor(out=t2[:], in0=t1[:], in1=d["u2"][:], op=ALU.mult)
-            t3 = pairp.tile([128, 8], F32, name="t3")
+            t3 = pairp.tile([128, n], F32, name="t3")
             nc.vector.reciprocal(out=t3[:], in_=t2[:])
-            cc = pairp.tile([128, 8], F32, name="cc")
-            nc.vector.scalar_tensor_tensor(out=cc[:], in0=t3[:], scalar=512.0 * math.log(2.0), in1=gainc[:, 8 * h:8 * h + 8], op0=ALU.mult, op1=ALU.mult)
-            ce = pairp.tile([128, 8, 32], F32, name="ce")
-            nc.vector.tensor_tensor(out=ce[:], in0=bc(cc[:]), in1=ecol[:].unsqueeze(1).to_broadcast([128, 8, 32]), op=ALU.mult)
-            r = ps.tile([128, 256], F32, name="sp")
+            cc = pairp.tile([128, n], F32, name="cc")
+            nc.vector.scalar_tensor_tensor(out=cc[:], in0=t3[:], scalar=512.0 * math.log(2.0), in1=gainc[:, lo:lo + n], op0=ALU.mult, op1=ALU.mult)
+            ce = pairp.tile([128, n, 32], F32, name="ce")
+            cb = cc[:].unsqueeze(2).to_broadcast([128, n, 32])
+            nc.vector.tensor_tensor(out=ce[:], in0=cb, in1=ecol[:].unsqueeze(1).to_broadcast([128, n, 32]), op=ALU.mult)
+            r = ps.tile([128, 32 * n], F32, name="sp")
             nc.tensor.matmul(r[:], lhsT=blk[:], rhs=ce[:].rearrange("p a i -> p (a i)"), start=True, stop=True)
-            d["cc"] = cc
-            d["cr"] = r
-
-        dt_ = {}
-
-        def pair5(h):
-            d = st[h]
-            z1 = pairp.tile([128, 8, 32], F32, name="z1")
-            nc.vector.tensor_tensor(out=z1[:], in0=d["cr"][:].rearrange("p (a i) -> p a i", i=32), in1=bc(d["cc"][:]), op=ALU.subtract)
-            z2 = pairp.tile([128, 8, 32], F32, name="z2")
+            z1 = pairp.tile([128, n, 32], F32, name="z1")
+            nc.vector.tensor_tensor(out=z1[:], in0=r[:].rearrange("p (a i) -> p a i", i=32), in1=cb, op=ALU.subtract)
+            z2 = pairp.tile([128, n, 32], F32, name="z2")
             nc.vector.tensor_tensor(out=z2[:], in0=z1[:], in1=d["kp"][:], op=ALU.mult)
-            de = pairp.tile([128, 8, 1], F32, name="de")
+            de = pairp.tile([128, n, 1], F32, name="de")
             nc.vector.tensor_reduce(out=de[:].rearrange("p a o -> p (a o)"), in_=z2[:], axis=AX.X, op=ALU.add)
             cur = de
             for k in range(3):
-                part = dparts[:, 8 * h:8 * h + 8, k:64:32]
-                nc.vector.tensor_copy(out=part, in_=cur[:].to_broadcast([128, 8, 2]))
+                nc.vector.tensor_copy(out=dparts[:, lo:lo + n, k:64:32], in_=cur[:].to_broadcast([128, n, 2]))
                 if k < 2:
-                    nxt = pairp.tile([128, 8, 1], F32, name="de%d" % k)
-                    nc.vector.tensor_tensor(out=nxt[:], in0=cur[:], in1=dparts[:, 8 * h:8 * h + 8, k:k + 1], op=ALU.subtract)
+                    nxt = pairp.tile([128, n, 1], F32, name="de%d" % k)
+                    nc.vector.tensor_tensor(out=nxt[:], in0=cur[:], in1=dparts[:, lo:lo + n, k:k + 1], op=ALU.subtract)
                     cur = nxt
-            t = ps.tile([128, 1024], BF16, name="sp")
-            for k in range(8):
-                nc.tensor.transpose(t[:, 128 * k:128 * k + 128], dparts[:, 8 * h + k, :], identb[:])
-            dt_[h] = t
-
-        dd = keep.tile([128, ROWS], BF16, name="dd")
-
-        def pair6(h):
-            nc.vector.tensor_copy(out=dd[:, 1024 * h:1024 * h + 1024], in_=dt_[h][:])
-
-        units = []
-        for b in range(NB):
-            for g in range(2):
-                if (b, g) in MPRIME:
-                    units.append((b, g, None))
+            for a0 in range(lo, lo + n, 8):
+                if a0 == lo:
+                    t = ps.tile([128, 1024], BF16, name="sp")
                 else:
-                    for k in range(4):
-                        units.append((b, g, k))
+                    t = pc.tile([128, 1024], BF16, name="c")
+                w = min(8, lo + n - a0)
+                for k in range(w):
+                    nc.tensor.transpose(t[:, 128 * k:128 * k + 128], dparts[:, a0 + k, :], identb[:])
+                nc.vector.tensor_copy(out=dd[:, 128 * a0:128 * (a0 + w)], in_=t[:, 0:128 * w])
+
+        chunks = []
+        for b in BORD:
+            w = CHUNK[b]
+            for k0 in range(0, 4, w):
+                chunks.append((b, k0, w))
+        units = []
+        for ch in chunks:
+            for g in range(2):
+                if (ch[0], g) in MPRIME:
+                    units.append((ch, g, None))
+                else:
+                    for k in range(ch[1], ch[1] + ch[2]):
+                        units.append((ch, g, k))
         cbank = {}
 
         def delta_c(i):
-            if i >= len(units):
+            if i >= len(units) or i in cbank:
                 return
-            b, g, k = units[i]
+            ch, g, k = units[i]
+            b, k0, w = ch
             if k is None and g == 1 and (b, 0) in MPRIME:
                 cbank[i] = cbank[i - 1]
                 return
             c0 = 512 * b
             if k is None:
-                t = pc.tile([128, 512], F32, name="c")
-                nc.tensor.matmul(t[:], lhsT=orow[:], rhs=dd[:, c0:c0 + 512], start=True, stop=True)
+                t = pc.tile([128, 128 * w], F32, name="c")
+                nc.tensor.matmul(t[:], lhsT=orow[:], rhs=dd[:, c0 + 128 * k0:c0 + 128 * (k0 + w)], start=True, stop=True)
             else:
                 t = pc.tile([128, 4, 128], F32, name="c")
                 for j in range(4):
@@ -465,82 +440,102 @@ def tile_smoothedrankdcginputgradient_kernel(tc, x, gamma, w1, g1, w2, gain, out
         dpi = {}
         dpc = {}
 
-        def m_prime(b, g):
+        def m_prime(b, g, eng):
+            assert ("n", b, 2 * g) in done and ("n", b, 2 * g + 1) in done
+            done.add(("m", b, g))
             for t in range(4):
-                hv = qn[b, g][:, t, :]
-                nc.scalar.activation(out=hv, in_=hv, func=ACT.Identity, scale=c8[:, 4 * g + t:4 * g + t + 1], bias=c8[:, 4 * g + t:4 * g + t + 1])
+                hv = hn[b, g][:, t, :]
+                cv = c8[:, 4 * g + t:4 * g + t + 1]
+                if eng == "s":
+                    nc.scalar.activation(out=hv, in_=hv, func=ACT.Identity, scale=cv, bias=cv)
+                elif eng == "v":
+                    nc.vector.tensor_scalar(out=hv, in0=hv, scalar1=cv, scalar2=cv, op0=ALU.mult, op1=ALU.add)
+                else:
+                    nc.gpsimd.tensor_scalar(out=hv, in0=hv, scalar1=cv, scalar2=cv, op0=ALU.mult, op1=ALU.add)
 
         def dp_op(i):
-            b, g, k = units[i]
-            if k is None or k == 0:
-                t = work.tile([128, 2048], BF16, name="dpi", align_bytes=64)
-                dpi[b, g] = t
+            ch, g, k = units[i]
+            b, k0, w = ch
+            assert ("n", b, 2 * g) in done and ("n", b, 2 * g + 1) in done and (k is not None or ("m", b, g) in done)
+            if k is None or k == k0:
+                t = work.tile([128, 512 * w], BF16, name="dpi", tag="il", bufs=ILBUF, align_bytes=64)
+                dpi[ch, g] = t
+            dst = dpi[ch, g]
             if k is None:
-                nc.vector.tensor_tensor(out=dpi[b, g][:].rearrange("p (r t) -> p r t", t=4), in0=qn[b, g][:].rearrange("p t r -> p r t"),
-                                        in1=cbank[i][:].unsqueeze(2).to_broadcast([128, 512, 4]), op=ALU.mult)
+                nc.vector.tensor_tensor(out=dst[:].rearrange("p (r t) -> p r t", t=4), in0=hn[b, g][:, :, 128 * k0:128 * (k0 + w)].rearrange("p t r -> p r t"),
+                                        in1=cbank[i][:].unsqueeze(2).to_broadcast([128, 128 * w, 4]), op=ALU.mult)
             else:
                 nc.vector.scalar_tensor_tensor(
-                    out=dpi[b, g][:, 512 * k:512 * k + 512].rearrange("p (r t) -> p r t", t=4),
-                    in0=qn[b, g][:, :, 128 * k:128 * k + 128].rearrange("p t r -> p r t"), scalar=1.0,
+                    out=dst[:, 512 * (k - k0):512 * (k - k0) + 512].rearrange("p (r t) -> p r t", t=4),
+                    in0=hn[b, g][:, :, 128 * k:128 * k + 128].rearrange("p t r -> p r t"), scalar=1.0,
                     in1=cbank[i][:].rearrange("p t r -> p r t"), op0=ALU.add, op1=ALU.mult)
 
-        def dp_quant(b, g):
-            c = work.tile([128, 512], U32, name="dpc", align_bytes=64, bufs=4)
-            s = work.tile([128, 512], U8, name="dps", align_bytes=64, bufs=4)
-            nc.vector.quantize_mx(out=c[:].bitcast(FP8X4), scales=s[:], in_=dpi[b, g][:])
-            dpc[b, g] = (c, s)
+        def dp_quant(ch, g):
+            w = ch[2]
+            c = work.tile([128, 128 * w], U32, name="dpc", tag="dpc", align_bytes=64, bufs=4)
+            s = work.tile([128, 128 * w], U8, name="dps", tag="dps", align_bytes=64, bufs=4)
+            nc.vector.quantize_mx(out=c[:].bitcast(FP8X4), scales=s[:], in_=dpi[ch, g][:])
+            dpc[ch, g] = (c, s)
 
         ysall = keep.tile([128, ROWS], U8, name="ysall", align_bytes=64)
         yt = {}
 
-        def stage2(b, t):
-            p = pp.tile([128, 512], F32, name="p")
+        def stage2(ch, t):
+            b, k0, w = ch
+            p = pp.tile([128, 128 * w], F32, name="p")
             for g in range(2):
-                c, s = dpc[b, g]
+                c, s = dpc[ch, g]
                 nc.tensor.matmul_mx(p[:], lhsT=wtc[:, g, 128 * t:128 * t + 128].bitcast(FP8X4), lhsT_scale=wts[:, g, 128 * t:128 * t + 128],
                                     rhs=c[:].bitcast(FP8X4), rhs_scale=s[:], start=(g == 0), stop=(g == 1))
             if t == 0:
-                y = work.tile([128, 4, 512], F32, name="yt")
-                yt[b] = y
-            nc.scalar.activation(out=yt[b][:, t, :], in_=p[:], func=ACT.Identity, scale=gmc[:, t:t + 1])
+                y = work.tile([128, 4, 128 * w], F32, name="yt", tag="yt" if w == 4 else "yh")
+                yt[ch] = y
+            if ID[b][t] == "s":
+                nc.scalar.activation(out=yt[ch][:, t, :], in_=p[:], func=ACT.Identity, scale=gmc[:, t:t + 1])
+            else:
+                nc.vector.tensor_scalar_mul(out=yt[ch][:, t, :], in0=p[:], scalar1=gmc[:, t:t + 1])
 
         yi = {}
 
-        def y_inter(b, eng):
-            t = work.tile([128, 2048], BF16, name="yi", align_bytes=64)
-            yi[b] = t
-            for k in range(2):
-                dst = t[:, 1024 * k:1024 * k + 1024].rearrange("p (r t) -> p r t", t=4)
-                src = yt[b][:, :, 256 * k:256 * k + 256].rearrange("p t r -> p r t")
-                if eng == "v":
-                    nc.vector.tensor_copy(out=dst, in_=src)
-                else:
-                    nc.gpsimd.tensor_scalar(out=dst, in0=src, scalar1=1.0, scalar2=0.0, op0=ALU.mult, op1=ALU.add)
+        def y_inter(ch, eng):
+            w = ch[2]
+            t = work.tile([128, 512 * w], BF16, name="yi", tag="il", bufs=ILBUF, align_bytes=64)
+            yi[ch] = t
+            dst = t[:].rearrange("p (r t) -> p r t", t=4)
+            src = yt[ch][:].rearrange("p t r -> p r t")
+            if eng == "v":
+                nc.vector.tensor_copy(out=dst, in_=src)
+            elif eng == "s":
+                nc.scalar.copy(out=dst, in_=src)
+            else:
+                nc.gpsimd.tensor_scalar(out=dst, in0=src, scalar1=1.0, scalar2=0.0, op0=ALU.mult, op1=ALU.add)
 
-        def y_quant(b):
-            c = work.tile([128, 512], U32, name="yc", align_bytes=64)
-            nc.vector.quantize_mx(out=c[:].bitcast(FP8X4), scales=ysall[:, 512 * b:512 * b + 512], in_=yi[b][:])
-            nc.sync.dma_start(out=words_out[0, :, 2048 * b:2048 * b + 2048].bitcast(I32), in_=c[:].bitcast(I32))
-            if b % 2 == 1:
-                c0 = 512 * (b - 1)
-                for q in range(4):
-                    nc.sync.dma_start(out=out_2[0, 4 * q:4 * q + 4, c0:c0 + 1024].bitcast(I32), in_=ysall[32 * q:32 * q + 4, c0:c0 + 1024].bitcast(I32))
+        def y_quant(ch):
+            b, k0, w = ch
+            c0 = 512 * b + 128 * k0
+            n = 128 * w
+            c = work.tile([128, n], U32, name="yc", tag="yc", align_bytes=64, bufs=3)
+            nc.vector.quantize_mx(out=c[:].bitcast(FP8X4), scales=ysall[:, c0:c0 + n], in_=yi[ch][:])
+            nc.sync.dma_start(out=words_out[0, :, 4 * c0:4 * (c0 + n)].bitcast(I32), in_=c[:].bitcast(I32))
+            for q in range(4):
+                nc.sync.dma_start(out=out_2[0, 4 * q:4 * q + 4, c0:c0 + n].bitcast(I32), in_=ysall[32 * q:32 * q + 4, c0:c0 + n].bitcast(I32))
 
         yo = {}
 
-        def y_turn(b, k):
+        def y_turn(ch, k):
             t = pt.tile([128, 4, 128], F32, name="tp")
             for j in range(4):
-                nc.tensor.transpose(t[:, j, :], yt[b][:, j, 128 * k:128 * k + 128], identf[:])
-            ttile["y", b, k] = t
+                nc.tensor.transpose(t[:, j, :], yt[ch][:, j, 128 * (k - ch[1]):128 * (k - ch[1]) + 128], identf[:])
+            ttile["y", ch, k] = t
 
-        def y_out(b, k, eng):
+        def y_out(ch, k, eng):
+            b = ch[0]
             if k % 2 == 0:
                 o = work.tile([128, 2, D], F32, name="yo", tag="io", bufs=4)
                 yo[b, k // 2] = o
             o = yo[b, k // 2]
             dst = o[:, k % 2, :].rearrange("p (m t) -> p m t", t=4)
-            src = ttile["y", b, k][:].rearrange("p t m -> p m t")
+            src = ttile["y", ch, k][:].rearrange("p t m -> p m t")
             if eng == "v":
                 nc.vector.tensor_copy(out=dst, in_=src)
             else:
@@ -555,64 +550,78 @@ def tile_smoothedrankdcginputgradient_kernel(tc, x, gamma, w1, g1, w2, gain, out
             beside.setdefault(i, []).append((fn, a))
 
         for b, s0 in zip((1, 2, 3), X_AT):
-            at(s0, x_mul, b, 0)
-            at(s0 + 1, x_turn, b, 0)
-            at(s0 + 1, x_mul, b, 1)
-            at(s0 + 3, x_copy, b, 0, "v")
-            at(s0 + 3, x_turn, b, 1)
-            at(s0 + 5, x_copy, b, 1, "v")
-            at(s0 + 6, x_quant, b)
+            for half in range(2):
+                at(s0 + XD * half, x_turn, b, half)
+                at(s0 + XD * half, x_copy, b, half)
+            at(s0 + XD, x_quant, b)
         at(12, consts)
-        at(2, c_rows)
-        for k in range(4):
-            at(4 * k + 5, q_op, 0, k)
-            at(4 * k + 6, n_op, 0, k)
-            at(26 + 2 * k, q_op, 1, 3 - k)
-            at(27 + 2 * k, n_op, 1, 3 - k)
-        for k in range(4):
-            at(40 + 2 * k + 2, n_op, 2, 3 - k)
-            at(56 + 2 * k + 2, n_gps if N3_GPS else n_op, 3, 3 - k)
-        for i, (g, half) in enumerate(((0, 0), (0, 1), (1, 0), (1, 1))):
-            at(WT_AT + 2 * i, wt_turn, g, half)
-            at(WT_AT + 1 + 2 * i, wt_copy, g, half)
-            if half == 1:
-                at(WT_AT + 2 + 2 * i, wt_quant, g)
-        for a0, fn in zip(PAIR_AT, (pair1, pair2, pair3a, pair3, pair4, pair5, pair6)):
-            at(a0, fn, 0)
-        for a0, fn in zip(PAIRB_AT, (pair1, pair2, pair3a, pair3, pair4, pair5, pair6)):
-            at(a0, fn, 1)
-
-        def unit(i):
-            b, g, k = units[i]
-            dp_op(i)
-            if k is None or k == 3:
-                dp_quant(b, g)
-            if i + 2 < 16 or i >= 16:
-                delta_c(i + 2)
-
-        for i in range(len(units)):
-            at(U_AT[i], unit, i)
-        at(U_AT[0] - 1, delta_c, 0)
-        at(U_AT[0] - 1, delta_c, 1)
-        at(U_AT[16] - 1, delta_c, 16)
-        at(U_AT[16] - 1, delta_c, 17)
-        for bg, a0 in MP_AT:
-            at(a0, m_prime, *bg)
-        for b in range(NB):
-            a0 = L_AT[b]
-            for t in range(4):
-                at(a0 + t, stage2, b, t)
-            at(a0 + 5, y_inter, b, YI[b])
-            at(a0 + 9, y_quant, b)
-            for k in range(4):
-                at(a0 + 4 + k, y_turn, b, k)
-                at(a0 + 4 + k, y_out, b, k, "s")
-
+        at(CR_AT, c_rows)
+        sig_at = {}
+        silu_at = {}
+        for i, (kind, b, ft) in enumerate(acts):
+            if kind == "silu":
+                silu_at[b, ft] = i
+            else:
+                sig_at[b, ft] = i
         for b in range(NB):
             for ft in range(8):
-                at(SW_AT[b][ft], s_weigh, b, ft)
-            at(ST_AT[b], s_turn, b)
-            at(ST_AT[b] + 1, s_sum, b)
+                at(silu_at[b, ft] + W_D, s_weigh, b, ft)
+            last = max(silu_at[b, ft] for ft in range(8)) + ST_D[b]
+            for k in range(4):
+                at(last + SS[b] * k // 2, s_turn, b, k)
+            at(last + SS[b] * 3 // 2, s_sum, b)
+            for k in range(4):
+                if acts[sig_at[b, 2 * k]][0] == "tanh":
+                    at(max(sig_at[b, 2 * k], sig_at[b, 2 * k + 1]) + 1, q_op, b, k)
+                at(max(sig_at[b, 2 * k], sig_at[b, 2 * k + 1], silu_at[b, 2 * k], silu_at[b, 2 * k + 1]) + N_D[b], n_op, b, k)
+        for i, (g, half) in enumerate(((0, 0), (0, 1), (1, 0), (1, 1))):
+            at(WT_AT[i], wt_turn, g, half)
+            at(WT_AT[i], wt_copy, g, half, WC[i])
+            if half == 1:
+                at(WT_AT[i], wt_quant, g)
+        for h, pos in enumerate(PAIR_AT):
+            at(pos[0], pair1, h)
+            at(pos[1], pair2, h)
+            at(pos[2], pair3, h)
+
+        first_of = []
+
+        def unit(i):
+            ch, g, k = units[i]
+            dp_op(i)
+            if k is None or k == ch[1] + ch[2] - 1:
+                dp_quant(ch, g)
+            if i + 2 not in first_of and i + 1 not in first_of:
+                delta_c(i + 2)
+
+        u_at = []
+        pos = 0
+        for ch, g, k in units:
+            if g == 0 and ch[1] == 0 and k in (None, 0):
+                pos = max(pos, U_AT[ch[0]])
+            u_at.append(pos)
+            pos += 1 if k is not None else ch[2]
+        for i in range(len(units)):
+            at(u_at[i], unit, i)
+        for grp in GROUPS:
+            i0 = min(i for i in range(len(units)) if units[i][0][0] in grp)
+            first_of.append(i0)
+            at(u_at[i0] - 1, delta_c, i0)
+            at(u_at[i0] - 1, delta_c, i0 + 1)
+        for bg, a0, eng in zip(MPRIME, MP_AT, MP_ENG):
+            at(a0, m_prime, bg[0], bg[1], eng)
+        for ch in chunks:
+            b = ch[0]
+            a0 = max(max(u_at[i] for i in range(len(units)) if units[i][0] == ch) + 1, len(acts) + L_P[BORD.index(b)])
+            sc = ch[2] / 4
+            for t in range(4):
+                at(a0 + int(sc * (L_D[0] + t)), stage2, ch, t)
+            at(a0 + int(sc * L_D[1]) + 1, y_inter, ch, YI[b])
+            at(a0 + int(sc * L_D[2]) + 2, y_quant, ch)
+            for k in range(ch[1], ch[1] + ch[2]):
+                at(a0 + int(sc * L_D[3]) + 1 + k - ch[1], y_turn, ch, k)
+                at(a0 + int(sc * L_D[3]) + 1 + k - ch[1], y_out, ch, k, YO[b][k])
+
         n_mm = 0
         for i in range(-1, max(beside) + 1):
             if 0 <= i < len(acts):
@@ -620,7 +629,5 @@ def tile_smoothedrankdcginputgradient_kernel(tc, x, gamma, w1, g1, w2, gain, out
             while n_mm < len(tiles) and (n_mm < PBUF or tiles[n_mm - PBUF][2] <= i):
                 stage1(n_mm)
                 n_mm += 1
-            if i < 0:
-                continue
             for fn, a in beside.get(i, []):
                 fn(*a)

import math
from contextlib import ExitStack

import concourse.mybir as mybir
from concourse.masks import make_identity

F32 = mybir.dt.float32
BF16 = mybir.dt.bfloat16
U32 = mybir.dt.uint32
I32 = mybir.dt.int32
U8 = mybir.dt.uint8
FP8X4 = mybir.dt.float8_e4m3fn_x4
ACT = mybir.ActivationFunctionType
ALU = mybir.AluOpType
AX = mybir.AxisListType

ROWS, D, F = 2048, 512, 1024
FLOPS = 4 * ROWS * D * F
NB = 4
BORD = (0, 1, 2, 3)
SWEEPS = (("mix", 0, 1), ("silu", 1, 1), ("sig", 1, -1), ("mix", 2, 1), ("silu", 3, 1), ("sig", 3, -1))
GROUPS = ((0, 1), (2, 3))
MPRIME = ((2, 1), (3, 0), (3, 1))
MP_ENG = "sss"
WEIGH = "vvvvsvgv"
HWBUF = 9
PBUF = 3
QBUF = 5
ILBUF = 5
CHUNK = (4, 4, 4, 2)
YI = "sssg"
SS = (1, 0, 1, 0)
ST_D = (3, 1, 3, 4)
N_D = (11, 9, 13, 18)
W_D = 1
L_P = (1, 7, 26, 31)
L_D = (2, 4, 6, 5)
YO = ("vsss", "ssss", "sssv", "sssv")
ID = ("ssss", "ssss", "ssss", "vvvs")
WI = "svgsvsss"
LO = "xywv"
NE = ("vvvv", "vvvv", "vvvv", "vvvv")
KP = "v"
WC = "vvvs"
MP_AT = (67, 84, 91)
PAIR_AT = ((31, 31, 31), (61, 62, 62))
CR_AT = 6
WT_AT = (41, 46, 48, 53)
X_AT = (7, 10, 29)
XD = 0
U_AT = (57, 68, 86, 80)


def tile_smoothedrankdcginputgradient_kernel(tc, x, gamma, w1, g1, w2, gain, out_0, out_1, out_2):
    nc = tc.nc
    xr = x.rearrange("q n d -> (q n) d")
    yr = out_0.rearrange("q n d -> (q n) d")
    words_out = out_1.rearrange("g p m t -> g p (m t)")

    with ExitStack() as ctx:
        keep = ctx.enter_context(tc.tile_pool(name="keep", bufs=1))
        work = ctx.enter_context(tc.tile_pool(name="work", bufs=2))
        pairp = ctx.enter_context(tc.tile_pool(name="pairp", bufs=1))
        pp = ctx.enter_context(tc.psum_pool(name="pp", bufs=PBUF))
        pt = ctx.enter_context(tc.psum_pool(name="pt", bufs=2))
        pc = ctx.enter_context(tc.psum_pool(name="pc", bufs=2))
        ps = ctx.enter_context(tc.psum_pool(name="ps", bufs=1))
        ctx.enter_context(tc.manual_schedule(engines={mybir.EngineType.Activation}))

        ones = keep.tile([128, 128], BF16, name="ones")
        nc.vector.memset(ones[:], 1.0)
        w1raw = keep.tile([128, 4, F], BF16, name="w1raw")
        xb = []
        for b in range(NB):
            xt = work.tile([128, 4, D], BF16, name="xt", tag="io", bufs=4)
            xb.append(xt)

        def load_x(b, half):
            r0 = 512 * b + 256 * half
            nc.sync.dma_start(out=xb[b][:, 2 * half:2 * half + 2, :], in_=xr[r0:r0 + 256, :].rearrange("(k p) d -> p k d", p=128))

        def load_w(g):
            nc.sync.dma_start(out=w1raw[:, :, 512 * g:512 * g + 512], in_=w1[:, 512 * g:512 * g + 512].rearrange("(p j) f -> p j f", j=4))

        for what in LO:
            if what in "xy":
                load_x(0, "xy".index(what))
            else:
                load_w("wv".index(what))
        gmb = keep.tile([128, 4], BF16, name="gmb")
        nc.scalar.dma_start(out=gmb[:], in_=gamma.rearrange("(p t) -> p t", t=4))
        g1b = keep.tile([128, 2, 4], BF16, name="g1b")
        nc.scalar.dma_start(out=g1b[:], in_=g1.rearrange("(g p t) -> p g t", g=2, t=4))
        w2b = keep.tile([128, 2, 4], BF16, name="w2b")
        nc.scalar.dma_start(out=w2b[:], in_=w2.rearrange("(g p t) -> p g t", g=2, t=4))
        for b in (1, 2, 3):
            load_x(b, 0)
            load_x(b, 1)

        identf = keep.tile([128, 128], F32, name="identf")
        make_identity(nc, identf[:])
        blk = keep.tile([128, 128], F32, name="blk")
        nc.gpsimd.memset(blk[:], 0.0)
        for q in range(4):
            nc.gpsimd.memset(blk[32 * q:32 * q + 32, 32 * q:32 * q + 32], 1.0)
        gainz = keep.tile([128, 128], BF16, name="gainz")
        nc.gpsimd.memset(gainz[:], 0.0)
        identb = keep.tile([128, 128], BF16, name="identb")
        nc.gpsimd.tensor_scalar(out=identb[:], in0=identf[:], scalar1=1.0, scalar2=0.0, op0=ALU.mult, op1=ALU.add)
        nc.sync.dma_start(out=gainz[0:16, :], in_=gain.rearrange("(a q) n -> a (q n)", q=4))
        crow = keep.tile([128, 8, 128], BF16, name="crow")
        cparts = keep.tile([128, 8, 128], BF16, name="cparts")
        nc.gpsimd.memset(cparts[:], 0.0)
        dparts = keep.tile([128, 16, 128], BF16, name="dparts")
        nc.gpsimd.memset(dparts[:], 0.0)
        orow = keep.tile([128, 128], BF16, name="orow")
        nc.gpsimd.memset(orow[:], 0.0)
        nc.gpsimd.memset(orow[0:32, :], 1.0)
        warm = keep.tile([128, 1], F32, name="warm")
        nc.scalar.activation(out=warm[:], in_=ones[:, 0:1], func=ACT.Sigmoid if SWEEPS[0][0] == "sig" else ACT.Silu)

        w1c = keep.tile([128, 2, 512], U32, name="w1c", align_bytes=64)
        w1s = keep.tile([128, 2, 512], U8, name="w1s", align_bytes=64)
        wtc = keep.tile([128, 2, 512], U32, name="wtc", align_bytes=64)
        wts = keep.tile([128, 2, 512], U8, name="wts", align_bytes=64)
        xc = []
        xs = []
        for b in range(NB):
            t1 = keep.tile([128, 512], U32, name="xc%d" % b, align_bytes=64)
            t2 = keep.tile([128, 512], U8, name="xs%d" % b, align_bytes=64)
            xc.append(t1)
            xs.append(t2)
        done = set()
        xg = {}
        xi = {}
        ttile = {}

        def x_turn(b, half):
            t = pt.tile([128, 2, 256], F32, name="tp")
            words = xb[b][:, 2 * half:2 * half + 2, :].bitcast(F32)
            for k in range(2):
                for u in range(2):
                    nc.tensor.transpose(t[:, u, 128 * k:128 * k + 128], words[:, k, u:256:2], identf[:])
            ttile[b, half] = t

        def x_copy(b, half):
            if half == 0:
                t = work.tile([128, 2048], BF16, name="xi", tag="il", bufs=ILBUF, align_bytes=64)
                xi[b] = t
            dst = xi[b][:, 1024 * half:1024 * half + 1024].rearrange("p (r u e) -> p r u e", u=2, e=2)
            src = ttile[b, half][:].bitcast(BF16).rearrange("p u (r e) -> p r u e", e=2)
            gam = gmb[:].rearrange("p (u e) -> p u e", e=2).unsqueeze(1).to_broadcast([128, 256, 2, 2])
            nc.vector.tensor_tensor(out=dst, in0=src, in1=gam, op=ALU.mult)

        def x_quant(b):
            nc.vector.quantize_mx(out=xc[b][:].bitcast(FP8X4), scales=xs[b][:], in_=xi[b][:])

        wi = {}

        def w_inter(g):
            t = work.tile([128, 2048], BF16, name="wi", tag="il", bufs=ILBUF, align_bytes=64)
            wi[g] = t
            dst = t[:].rearrange("p (t m j) -> p t m j", t=4, j=4)
            src = w1raw[:, :, 512 * g:512 * g + 512].rearrange("p j (m t) -> p t m j", t=4)
            for t2 in range(4):
                eng = WI[4 * g + t2]
                if eng == "v":
                    nc.vector.tensor_copy(out=dst[:, t2, :, :], in_=src[:, t2, :, :])
                elif eng == "s":
                    nc.scalar.copy(out=dst[:, t2, :, :], in_=src[:, t2, :, :])
                else:
                    nc.gpsimd.tensor_scalar(out=dst[:, t2, :, :], in0=src[:, t2, :, :], scalar1=1.0, scalar2=0.0, op0=ALU.mult, op1=ALU.add)

        def w_quant(g):
            nc.vector.quantize_mx(out=w1c[:, g, :].bitcast(FP8X4), scales=w1s[:, g, :], in_=wi[g][:])

        def wt_turn(g, half):
            t = pt.tile([128, 2, 2, 128], F32, name="tp")
            for k in range(2):
                words = w1raw[:, 2 * half + k, :].bitcast(F32)
                for u in range(2):
                    nc.tensor.transpose(t[:, k, u, :], words[:, 256 * g + u:256 * g + 256:2], identf[:])
            ttile["w", g, half] = t

        def wt_copy(g, half, eng):
            if half == 0:
                t = work.tile([128, 2048], BF16, name="wi", tag="il", bufs=ILBUF, align_bytes=64)
                wi["t", g] = t
            dst = wi["t", g][:, 1024 * half:1024 * half + 1024].bitcast(F32).rearrange("p (k m u) -> p k m u", k=2, u=2)
            src = ttile["w", g, half][:].rearrange("p k u m -> p k m u")
            if eng == "v":
                nc.vector.tensor_copy(out=dst, in_=src)
            else:
                nc.scalar.copy(out=dst, in_=src)

        def wt_quant(g):
            nc.vector.quantize_mx(out=wtc[:, g, :].bitcast(FP8X4), scales=wts[:, g, :], in_=wi["t", g][:])

        x_turn(0, 0)
        x_copy(0, 0)
        x_turn(0, 1)
        x_copy(0, 1)
        w_inter(0)
        x_quant(0)
        w_quant(0)
        w_inter(1)
        g1c = keep.tile([128, 8], F32, name="g1c")
        nc.vector.tensor_copy(out=g1c[:], in_=g1b[:].rearrange("p g t -> p (g t)"))
        ng1c = keep.tile([128, 8], F32, name="ng1c")
        nc.vector.tensor_scalar_mul(out=ng1c[:], in0=g1c[:], scalar1=-1.0)
        hg1c = keep.tile([128, 8], F32, name="hg1c")
        nc.vector.tensor_scalar_mul(out=hg1c[:], in0=g1c[:], scalar1=0.5)
        w_quant(1)
        w2c = keep.tile([128, 8], F32, name="w2c")
        nc.vector.tensor_copy(out=w2c[:], in_=w2b[:].rearrange("p g t -> p (g t)"))
        gmc = keep.tile([128, 4], F32, name="gmc")
        nc.vector.tensor_copy(out=gmc[:], in_=gmb[:])
        c8 = keep.tile([128, 8], F32, name="c8")
        nc.vector.tensor_tensor(out=c8[:], in0=g1c[:], in1=w2c[:], op=ALU.mult)

        ecol = keep.tile([128, 32], F32, name="ecol")
        gainc = keep.tile([128, 16], F32, name="gainc")

        def consts():
            nc.vector.tensor_reduce(out=ecol[:], in_=identf[:].rearrange("p (a i) -> p i a", i=32), axis=AX.X, op=ALU.add)
            t = pt.tile([128, 128], BF16, name="tp")
            nc.tensor.transpose(t[:], gainz[:], identb[:])
            nc.vector.tensor_copy(out=gainc[:], in_=t[:, 0:16])

        def c_rows():
            c_hi = keep.tile([128, 8, 1], BF16, name="c_hi")
            cv = c8[:].unsqueeze(2)
            nc.vector.tensor_copy(out=c_hi[:], in_=cv)
            nc.vector.tensor_copy(out=cparts[:, :, 0:3], in_=c_hi[:].to_broadcast([128, 8, 3]))
            nc.vector.tensor_tensor(out=cparts[:, :, 32:35], in0=cv.to_broadcast([128, 8, 3]), in1=c_hi[:].to_broadcast([128, 8, 3]), op=ALU.subtract)
            t = pt.tile([128, 8, 128], BF16, name="tp")
            for j in range(8):
                nc.tensor.transpose(t[:, j, :], cparts[:, j, :], identb[:])
            nc.scalar.copy(out=crow[:], in_=t[:])

        acts = []
        for kind, b, order in SWEEPS:
            for ft in range(8)[::order]:
                if kind == "mix":
                    acts.append(("silu", b, ft))
                    acts.append(("tanh", b, ft))
                else:
                    acts.append((kind, b, ft))
        tiles = []
        where = {}
        for i, (kind, b, ft) in enumerate(acts):
            kept = ft >= 8 - PBUF or (i and acts[i - 1][1:] == (b, ft))
            if (b, ft) in where and kept and i - tiles[where[b, ft]][2] <= 2 * PBUF:
                m = where[b, ft]
                tiles[m] = (b, ft, i)
            else:
                where[b, ft] = len(tiles)
                tiles.append((b, ft, i))
        acc = {}

        def stage1(m):
            b, ft, last = tiles[m]
            g, t = divmod(ft, 4)
            p = pp.tile([128, 512], F32, name="p")
            nc.tensor.matmul_mx(p[:], lhsT=w1c[:, g, 128 * t:128 * t + 128].bitcast(FP8X4), lhsT_scale=w1s[:, g, 128 * t:128 * t + 128],
                                rhs=xc[b][:].bitcast(FP8X4), rhs_scale=xs[b][:], start=True, stop=True)
            acc[b, ft] = p

        hn = {}
        qn = {}

        def act(i):
            kind, b, ft = acts[i]
            g, t = divmod(ft, 4)
            if kind == "silu":
                if (b, g) not in hn:
                    h_t = work.tile([128, 4, 512], F32, name="h", bufs=8)
                    hn[b, g] = h_t
                nc.scalar.activation(out=hn[b, g][:, t, :], in_=acc[b, ft][:], func=ACT.Silu, scale=g1c[:, ft:ft + 1])
                return
            if (b, ft // 2) not in qn:
                q = work.tile([128, 2, 512], F32, name="q", bufs=QBUF)
                qn[b, ft // 2] = q
            dst = qn[b, ft // 2][:, ft % 2, :]
            if kind == "tanh":
                nc.scalar.activation(out=dst, in_=acc[b, ft][:], func=ACT.Tanh, scale=hg1c[:, ft:ft + 1])
            else:
                nc.scalar.activation(out=dst, in_=acc[b, ft][:], func=ACT.Sigmoid, scale=ng1c[:, ft:ft + 1])

        def q_op(b, k):
            q = qn[b, k][:]
            nc.vector.tensor_scalar(out=q, in0=q, scalar1=-0.5, scalar2=0.5, op0=ALU.mult, op1=ALU.add)
            done.add(("q", b, k))

        def n_op(b, k):
            g, t = divmod(2 * k, 4)
            hv = hn[b, g][:, t:t + 2, :]
            assert ("w", b, 2 * k) in done and ("w", b, 2 * k + 1) in done
            done.add(("n", b, k))
            if NE[b][k] == "v":
                nc.vector.scalar_tensor_tensor(out=hv, in0=hv, scalar=1.0, in1=qn[b, k][:], op0=ALU.subtract, op1=ALU.mult)
            else:
                nc.gpsimd.tensor_scalar(out=hv, in0=hv, scalar1=1.0, scalar2=-1.0, op0=ALU.mult, op1=ALU.add)
                nc.gpsimd.tensor_tensor(out=hv, in0=hv, in1=qn[b, k][:], op=ALU.mult)

        sps = {}

        hw = {}

        def s_weigh(b, ft):
            g, t = divmod(ft, 4)
            w_t = work.tile([128, 512], F32, name="hw", bufs=HWBUF)
            if WEIGH[ft] == "v":
                nc.vector.tensor_scalar_mul(out=w_t[:], in0=hn[b, g][:, t, :], scalar1=w2c[:, ft:ft + 1])
            elif WEIGH[ft] == "s":
                nc.scalar.mul(out=w_t[:], in_=hn[b, g][:, t, :], mul=w2c[:, ft:ft + 1])
            else:
                nc.gpsimd.tensor_scalar(out=w_t[:], in0=hn[b, g][:, t, :], scalar1=w2c[:, ft:ft + 1], scalar2=0.0, op0=ALU.mult, op1=ALU.add)
            hw[b, ft] = w_t
            done.add(("w", b, ft))

        def s_turn(b, k):
            if k == 0:
                t = ps.tile([128, 4, 128], F32, name="sp")
                sps[b] = t
            for ft in range(8):
                nc.tensor.matmul(sps[b][:, k, :], lhsT=hw[b, ft][:, 128 * k:128 * k + 128], rhs=identf[:], start=(ft == 0), stop=(ft == 7), is_transpose=True)

        s_all = keep.tile([128, 16], F32, name="s_all")

        def s_sum(b):
            nc.vector.tensor_reduce(out=s_all[:, 4 * b:4 * b + 4], in_=sps[b][:], axis=AX.X, op=ALU.add)
            done.add(("sum", b))

        st = {}
        dd = keep.tile([128, ROWS], BF16, name="dd")

        def pair1(h):
            lo, n = 4 * GROUPS[h][0], 4 * len(GROUPS[h])
            assert all(("sum", b) in done for b in GROUPS[h])
            s = s_all[:, lo:lo + n]
            se = pairp.tile([128, n, 32], F32, name="se")
            nc.vector.tensor_tensor(out=se[:], in0=s.unsqueeze(2).to_broadcast([128, n, 32]), in1=ecol[:].unsqueeze(1).to_broadcast([128, n, 32]), op=ALU.mult)
            r = ps.tile([128, 32 * n], F32, name="sp")
            nc.tensor.matmul(r[:], lhsT=blk[:], rhs=se[:].rearrange("p a i -> p (a i)"), start=True, stop=True)
            df = pairp.tile([128, n, 32], F32, name="df")
            nc.vector.tensor_tensor(out=df[:], in0=r[:].rearrange("p (a i) -> p a i", i=32), in1=s.unsqueeze(2).to_broadcast([128, n, 32]), op=ALU.subtract)
            st[h] = {"df": df, "n": n, "lo": lo}

        def pair2(h):
            d = st[h]
            kk = pairp.tile([128, d["n"], 32], F32, name="kk")
            nc.scalar.activation(out=kk[:], in_=d["df"][:], func=ACT.Sigmoid, scale=2.0)
            kn = pairp.tile([128, d["n"], 32], F32, name="kn")
            nc.scalar.activation(out=kn[:], in_=d["df"][:], func=ACT.Sigmoid, scale=-2.0)
            u = pairp.tile([128, d["n"]], F32, name="u")
            nc.vector.tensor_reduce(out=u[:], in_=kk[:], axis=AX.X, op=ALU.add)
            u2 = pairp.tile([128, d["n"]], F32, name="u2")
            nc.vector.tensor_scalar_add(out=u2[:], in0=u[:], scalar1=1.5)
            kp = pairp.tile([128, d["n"], 32], F32, name="kp")
            eng = nc.vector if KP == "v" else nc.gpsimd
            eng.tensor_tensor(out=kp[:], in0=kk[:], in1=kn[:], op=ALU.mult)
            d["u2"] = u2
            d["kp"] = kp

        def pair3(h):
            d = st[h]
            n, lo = d["n"], d["lo"]
            ln = pairp.tile([128, n], F32, name="ln")
            nc.scalar.activation(out=ln[:], in_=d["u2"][:], func=ACT.Ln)
            t1 = pairp.tile([128, n], F32, name="t1")
            nc.vector.tensor_tensor(out=t1[:], in0=ln[:], in1=ln[:], op=ALU.mult)
            t2 = pairp.tile([128, n], F32, name="t2")
            nc.vector.tensor_tensor(out=t2[:], in0=t1[:], in1=d["u2"][:], op=ALU.mult)
            t3 = pairp.tile([128, n], F32, name="t3")
            nc.vector.reciprocal(out=t3[:], in_=t2[:])
            cc = pairp.tile([128, n], F32, name="cc")
            nc.vector.scalar_tensor_tensor(out=cc[:], in0=t3[:], scalar=512.0 * math.log(2.0), in1=gainc[:, lo:lo + n], op0=ALU.mult, op1=ALU.mult)
            ce = pairp.tile([128, n, 32], F32, name="ce")
            cb = cc[:].unsqueeze(2).to_broadcast([128, n, 32])
            nc.vector.tensor_tensor(out=ce[:], in0=cb, in1=ecol[:].unsqueeze(1).to_broadcast([128, n, 32]), op=ALU.mult)
            r = ps.tile([128, 32 * n], F32, name="sp")
            nc.tensor.matmul(r[:], lhsT=blk[:], rhs=ce[:].rearrange("p a i -> p (a i)"), start=True, stop=True)
            z1 = pairp.tile([128, n, 32], F32, name="z1")
            nc.vector.tensor_tensor(out=z1[:], in0=r[:].rearrange("p (a i) -> p a i", i=32), in1=cb, op=ALU.subtract)
            z2 = pairp.tile([128, n, 32], F32, name="z2")
            nc.vector.tensor_tensor(out=z2[:], in0=z1[:], in1=d["kp"][:], op=ALU.mult)
            de = pairp.tile([128, n, 1], F32, name="de")
            nc.vector.tensor_reduce(out=de[:].rearrange("p a o -> p (a o)"), in_=z2[:], axis=AX.X, op=ALU.add)
            cur = de
            for k in range(3):
                nc.vector.tensor_copy(out=dparts[:, lo:lo + n, k:64:32], in_=cur[:].to_broadcast([128, n, 2]))
                if k < 2:
                    nxt = pairp.tile([128, n, 1], F32, name="de%d" % k)
                    nc.vector.tensor_tensor(out=nxt[:], in0=cur[:], in1=dparts[:, lo:lo + n, k:k + 1], op=ALU.subtract)
                    cur = nxt
            for a0 in range(lo, lo + n, 8):
                if a0 == lo:
                    t = ps.tile([128, 1024], BF16, name="sp")
                else:
                    t = pc.tile([128, 1024], BF16, name="c")
                w = min(8, lo + n - a0)
                for k in range(w):
                    nc.tensor.transpose(t[:, 128 * k:128 * k + 128], dparts[:, a0 + k, :], identb[:])
                nc.vector.tensor_copy(out=dd[:, 128 * a0:128 * (a0 + w)], in_=t[:, 0:128 * w])

        chunks = []
        for b in BORD:
            w = CHUNK[b]
            for k0 in range(0, 4, w):
                chunks.append((b, k0, w))
        units = []
        for ch in chunks:
            for g in range(2):
                if (ch[0], g) in MPRIME:
                    units.append((ch, g, None))
                else:
                    for k in range(ch[1], ch[1] + ch[2]):
                        units.append((ch, g, k))
        cbank = {}

        def delta_c(i):
            if i >= len(units) or i in cbank:
                return
            ch, g, k = units[i]
            b, k0, w = ch
            if k is None and g == 1 and (b, 0) in MPRIME:
                cbank[i] = cbank[i - 1]
                return
            c0 = 512 * b
            if k is None:
                t = pc.tile([128, 128 * w], F32, name="c")
                nc.tensor.matmul(t[:], lhsT=orow[:], rhs=dd[:, c0 + 128 * k0:c0 + 128 * (k0 + w)], start=True, stop=True)
            else:
                t = pc.tile([128, 4, 128], F32, name="c")
                for j in range(4):
                    nc.tensor.matmul(t[:, j, :], lhsT=crow[:, 4 * g + j, :], rhs=dd[:, c0 + 128 * k:c0 + 128 * k + 128], start=True, stop=True)
            cbank[i] = t

        dpi = {}
        dpc = {}

        def m_prime(b, g, eng):
            assert ("n", b, 2 * g) in done and ("n", b, 2 * g + 1) in done
            done.add(("m", b, g))
            for t in range(4):
                hv = hn[b, g][:, t, :]
                cv = c8[:, 4 * g + t:4 * g + t + 1]
                if eng == "s":
                    nc.scalar.activation(out=hv, in_=hv, func=ACT.Identity, scale=cv, bias=cv)
                elif eng == "v":
                    nc.vector.tensor_scalar(out=hv, in0=hv, scalar1=cv, scalar2=cv, op0=ALU.mult, op1=ALU.add)
                else:
                    nc.gpsimd.tensor_scalar(out=hv, in0=hv, scalar1=cv, scalar2=cv, op0=ALU.mult, op1=ALU.add)

        def dp_op(i):
            ch, g, k = units[i]
            b, k0, w = ch
            assert ("n", b, 2 * g) in done and ("n", b, 2 * g + 1) in done and (k is not None or ("m", b, g) in done)
            if k is None or k == k0:
                t = work.tile([128, 512 * w], BF16, name="dpi", tag="il", bufs=ILBUF, align_bytes=64)
                dpi[ch, g] = t
            dst = dpi[ch, g]
            if k is None:
                nc.vector.tensor_tensor(out=dst[:].rearrange("p (r t) -> p r t", t=4), in0=hn[b, g][:, :, 128 * k0:128 * (k0 + w)].rearrange("p t r -> p r t"),
                                        in1=cbank[i][:].unsqueeze(2).to_broadcast([128, 128 * w, 4]), op=ALU.mult)
            else:
                nc.vector.scalar_tensor_tensor(
                    out=dst[:, 512 * (k - k0):512 * (k - k0) + 512].rearrange("p (r t) -> p r t", t=4),
                    in0=hn[b, g][:, :, 128 * k:128 * k + 128].rearrange("p t r -> p r t"), scalar=1.0,
                    in1=cbank[i][:].rearrange("p t r -> p r t"), op0=ALU.add, op1=ALU.mult)

        def dp_quant(ch, g):
            w = ch[2]
            c = work.tile([128, 128 * w], U32, name="dpc", tag="dpc", align_bytes=64, bufs=4)
            s = work.tile([128, 128 * w], U8, name="dps", tag="dps", align_bytes=64, bufs=4)
            nc.vector.quantize_mx(out=c[:].bitcast(FP8X4), scales=s[:], in_=dpi[ch, g][:])
            dpc[ch, g] = (c, s)

        ysall = keep.tile([128, ROWS], U8, name="ysall", align_bytes=64)
        yt = {}

        def stage2(ch, t):
            b, k0, w = ch
            p = pp.tile([128, 128 * w], F32, name="p")
            for g in range(2):
                c, s = dpc[ch, g]
                nc.tensor.matmul_mx(p[:], lhsT=wtc[:, g, 128 * t:128 * t + 128].bitcast(FP8X4), lhsT_scale=wts[:, g, 128 * t:128 * t + 128],
                                    rhs=c[:].bitcast(FP8X4), rhs_scale=s[:], start=(g == 0), stop=(g == 1))
            if t == 0:
                y = work.tile([128, 4, 128 * w], F32, name="yt", tag="yt" if w == 4 else "yh")
                yt[ch] = y
            if ID[b][t] == "s":
                nc.scalar.activation(out=yt[ch][:, t, :], in_=p[:], func=ACT.Identity, scale=gmc[:, t:t + 1])
            else:
                nc.vector.tensor_scalar_mul(out=yt[ch][:, t, :], in0=p[:], scalar1=gmc[:, t:t + 1])

        yi = {}

        def y_inter(ch, eng):
            w = ch[2]
            t = work.tile([128, 512 * w], BF16, name="yi", tag="il", bufs=ILBUF, align_bytes=64)
            yi[ch] = t
            dst = t[:].rearrange("p (r t) -> p r t", t=4)
            src = yt[ch][:].rearrange("p t r -> p r t")
            if eng == "v":
                nc.vector.tensor_copy(out=dst, in_=src)
            elif eng == "s":
                nc.scalar.copy(out=dst, in_=src)
            else:
                nc.gpsimd.tensor_scalar(out=dst, in0=src, scalar1=1.0, scalar2=0.0, op0=ALU.mult, op1=ALU.add)

        def y_quant(ch):
            b, k0, w = ch
            c0 = 512 * b + 128 * k0
            n = 128 * w
            c = work.tile([128, n], U32, name="yc", tag="yc", align_bytes=64, bufs=3)
            nc.vector.quantize_mx(out=c[:].bitcast(FP8X4), scales=ysall[:, c0:c0 + n], in_=yi[ch][:])
            nc.sync.dma_start(out=words_out[0, :, 4 * c0:4 * (c0 + n)].bitcast(I32), in_=c[:].bitcast(I32))
            for q in range(4):
                nc.sync.dma_start(out=out_2[0, 4 * q:4 * q + 4, c0:c0 + n].bitcast(I32), in_=ysall[32 * q:32 * q + 4, c0:c0 + n].bitcast(I32))

        yo = {}

        def y_turn(ch, k):
            t = pt.tile([128, 4, 128], F32, name="tp")
            for j in range(4):
                nc.tensor.transpose(t[:, j, :], yt[ch][:, j, 128 * (k - ch[1]):128 * (k - ch[1]) + 128], identf[:])
            ttile["y", ch, k] = t

        def y_out(ch, k, eng):
            b = ch[0]
            if k % 2 == 0:
                o = work.tile([128, 2, D], F32, name="yo", tag="io", bufs=4)
                yo[b, k // 2] = o
            o = yo[b, k // 2]
            dst = o[:, k % 2, :].rearrange("p (m t) -> p m t", t=4)
            src = ttile["y", ch, k][:].rearrange("p t m -> p m t")
            if eng == "v":
                nc.vector.tensor_copy(out=dst, in_=src)
            else:
                nc.scalar.copy(out=dst, in_=src)
            if k % 2 == 1:
                r0 = 512 * b + 128 * (k - 1)
                nc.sync.dma_start(out=yr[r0:r0 + 256, :].rearrange("(k p) d -> p k d", p=128), in_=o[:])

        beside = {}

        def at(i, fn, *a):
            beside.setdefault(i, []).append((fn, a))

        for b, s0 in zip((1, 2, 3), X_AT):
            for half in range(2):
                at(s0 + XD * half, x_turn, b, half)
                at(s0 + XD * half, x_copy, b, half)
            at(s0 + XD, x_quant, b)
        at(12, consts)
        at(CR_AT, c_rows)
        sig_at = {}
        silu_at = {}
        for i, (kind, b, ft) in enumerate(acts):
            if kind == "silu":
                silu_at[b, ft] = i
            else:
                sig_at[b, ft] = i
        for b in range(NB):
            for ft in range(8):
                at(silu_at[b, ft] + W_D, s_weigh, b, ft)
            last = max(silu_at[b, ft] for ft in range(8)) + ST_D[b]
            for k in range(4):
                at(last + SS[b] * k // 2, s_turn, b, k)
            at(last + SS[b] * 3 // 2, s_sum, b)
            for k in range(4):
                if acts[sig_at[b, 2 * k]][0] == "tanh":
                    at(max(sig_at[b, 2 * k], sig_at[b, 2 * k + 1]) + 1, q_op, b, k)
                at(max(sig_at[b, 2 * k], sig_at[b, 2 * k + 1], silu_at[b, 2 * k], silu_at[b, 2 * k + 1]) + N_D[b], n_op, b, k)
        for i, (g, half) in enumerate(((0, 0), (0, 1), (1, 0), (1, 1))):
            at(WT_AT[i], wt_turn, g, half)
            at(WT_AT[i], wt_copy, g, half, WC[i])
            if half == 1:
                at(WT_AT[i], wt_quant, g)
        for h, pos in enumerate(PAIR_AT):
            at(pos[0], pair1, h)
            at(pos[1], pair2, h)
            at(pos[2], pair3, h)

        first_of = []

        def unit(i):
            ch, g, k = units[i]
            dp_op(i)
            if k is None or k == ch[1] + ch[2] - 1:
                dp_quant(ch, g)
            if i + 2 not in first_of and i + 1 not in first_of:
                delta_c(i + 2)

        u_at = []
        pos = 0
        for ch, g, k in units:
            if g == 0 and ch[1] == 0 and k in (None, 0):
                pos = max(pos, U_AT[ch[0]])
            u_at.append(pos)
            pos += 1 if k is not None else ch[2]
        for i in range(len(units)):
            at(u_at[i], unit, i)
        for grp in GROUPS:
            i0 = min(i for i in range(len(units)) if units[i][0][0] in grp)
            first_of.append(i0)
            at(u_at[i0] - 1, delta_c, i0)
            at(u_at[i0] - 1, delta_c, i0 + 1)
        for bg, a0, eng in zip(MPRIME, MP_AT, MP_ENG):
            at(a0, m_prime, bg[0], bg[1], eng)
        for ch in chunks:
            b = ch[0]
            a0 = max(max(u_at[i] for i in range(len(units)) if units[i][0] == ch) + 1, len(acts) + L_P[BORD.index(b)])
            sc = ch[2] / 4
            for t in range(4):
                at(a0 + int(sc * (L_D[0] + t)), stage2, ch, t)
            at(a0 + int(sc * L_D[1]) + 1, y_inter, ch, YI[b])
            at(a0 + int(sc * L_D[2]) + 2, y_quant, ch)
            for k in range(ch[1], ch[1] + ch[2]):
                at(a0 + int(sc * L_D[3]) + 1 + k - ch[1], y_turn, ch, k)
                at(a0 + int(sc * L_D[3]) + 1 + k - ch[1], y_out, ch, k, YO[b][k])

        n_mm = 0
        for i in range(-1, max(beside) + 1):
            if 0 <= i < len(acts):
                act(i)
            while n_mm < len(tiles) and (n_mm < PBUF or tiles[n_mm - PBUF][2] <= i):
                stage1(n_mm)
                n_mm += 1
            for fn, a in beside.get(i, []):
                fn(*a)
